import numpy as np, ml_dtypes
CORES = [8,136,40,168]
N = 4
BF = ml_dtypes.bfloat16
def gentries(a):
    return np.ascontiguousarray(a.reshape(8, 16, -1).transpose(0, 2, 1)).reshape(8, -1)
def gtable(e):
    e = np.asarray(e); return np.ascontiguousarray(e.reshape(8, -1, 16).transpose(0, 2, 1)).reshape(128, -1).astype(np.int32)
W, LV, B, NB, Q, C = 64, 4, 128, 8, 4, 5440
K = NB * Q
SMIN, SMAX, DM, SH = 4, 56, 12, 9
CUTS = np.array([12, 24, 48]); BASE = np.array([0, 4096, 5120, 5376])
def tobf(v):
    return v.astype(np.float32).astype(BF)
def tolists(v):
    return np.stack([gtable(u) for u in v])
def tobox(x, y, s):
    return np.stack([x, y, s], axis=2).reshape(N, 8, 3 * B).astype(np.int32)
def setup_inputs(rng):
    v = rng.integers(0, 256, (N, 128, C), dtype=np.uint8) & rng.integers(0, 256, (N, 128, C), dtype=np.uint8)
    w = rng.integers(-8, 9, (N, 128, 3, NB // 2)); w = np.concatenate([w, -w], axis=3).reshape(N, 128, 3 * NB)
    n = np.arange(K) // Q; hb = 64 // NB
    sx = 4 * (n % 4) + rng.integers(0, 4, (N, 8, K)); sy = hb * (n // 4) + rng.integers(0, hb, (N, 8, K))
    lo = np.append(SMIN, CUTS); hi = np.append(CUTS - 1, SMAX); l = rng.integers(0, LV, (N, 8, B))
    s = rng.integers(lo[l], hi[l] + 1); x = rng.integers(0, W - s + 1); y = rng.integers(0, W - s + 1)
    return {"pyr": tobf(v), "head": tobf(w), "sx": tolists(sx), "sy": tolists(sy), "box": tobox(x, y, s)}
def setup_inputs_ends(rng):
    d = setup_inputs(rng); E = np.concatenate([[SMIN, SMAX], CUTS, CUTS - 1])
    s = E[(np.arange(B) + np.arange(8)[:, None] + np.arange(N)[:, None, None]) % len(E)]
    d["box"] = tobox((W - s) * rng.integers(0, 2, s.shape), (W - s) * rng.integers(0, 2, s.shape), s)
    d["sx"] = tolists(15 * rng.integers(0, 2, (N, 8, K))); d["sy"] = tolists(15 * rng.integers(0, 2, (N, 8, K))); return d
def setup_inputs_slow(rng):
    d = setup_inputs(rng); w = np.zeros((N, 8, 16, 3, NB)); i = np.arange(N)[:, None, None]; g = np.arange(8)[:, None]; c = np.arange(3)
    w[i, g, rng.integers(0, 16, (N, 8, 3)), c, rng.integers(0, NB, (N, 8, 3))] = np.array([-8, -1, 1, 8])[(i + g + c) % 4]
    d["head"] = tobf(w.reshape(N, 128, 3 * NB)); return d
def setup_inputs_twins(rng):
    d = setup_inputs(rng); b = d["box"].reshape(N, 8, 3, B)
    d["box"] = np.ascontiguousarray(np.broadcast_to(b[..., :1], b.shape)).reshape(N, 8, 3 * B); return d
def setup_inputs_push(rng):
    d = setup_inputs(rng); g = 8 * rng.choice(np.array([-1, 1]), (N, 8, 1, 3, 1)); g[:, 0] = 8; g[:, 1] = -8
    d["head"] = tobf(np.broadcast_to(g, (N, 8, 16, 3, NB)).reshape(N, 128, 3 * NB)); return d
def setup_inputs_spread(rng):
    d = setup_inputs(rng); v = np.minimum(rng.integers(0, 256, (N, 8, 16, C), dtype=np.uint8), rng.integers(0, 256, (N, 8, 1, C), dtype=np.uint8))
    d["pyr"] = tobf(v.reshape(N, 128, C)); w = rng.integers(-8, 9, (N, 128, 3 * NB)); d["head"] = tobf(w * (rng.random(w.shape) < 0.25))
    d["sx"] = tolists(rng.integers(0, 16, (N, 8, K))); d["sy"] = tolists(rng.integers(0, 16, (N, 8, K))); return d
def check_inputs(d):
    bad = []
    v = d["pyr"].astype(np.float32)
    if not np.all((v >= 0) & (v <= 255) & (v == np.floor(v))): bad.append("pyr")
    v = d["head"].astype(np.float32)
    if not np.all((v >= -8) & (v <= 8) & (v == np.floor(v))): bad.append("head")
    for a in ("sx", "sy"):
        if not np.all((d[a] >= 0) & (d[a] <= 15)): bad.append(a)
    b = d["box"].astype(np.int64).reshape(N, 8, 3, B); x, y, s = b[:, :, 0], b[:, :, 1], b[:, :, 2]
    if not np.all((s >= SMIN) & (s <= SMAX)): bad.append("size")
    if not np.all((x >= 0) & (y >= 0) & (x + s <= W) & (y + s <= W)): bad.append("box")
    return bad
def reference(pyr, head, sx, sy, box):
    P = [pyr[q].astype(np.float32).reshape(8, 16, C) for q in range(N)]
    H = [head[q].astype(np.float32).astype(np.int64).reshape(8, 16, 3, NB) for q in range(N)]
    ax = [gentries(sx[q]).astype(np.int64)[:, None, :] for q in range(N)]; ay = [gentries(sy[q]).astype(np.int64)[:, None, :] for q in range(N)]
    feat = np.zeros((N, 128, NB * B), BF); trail = np.zeros((N, 8, N, 3, B), np.float32)
    g = np.arange(8)[:, None, None]; ch = np.arange(16)[None, :, None]
    for r in range(N):
        b = box[r].astype(np.int64).reshape(8, 3, B); x, y, s = b[:, 0], b[:, 1], b[:, 2]
        for h in range(N):
            q = (r + h) % N
            l = np.zeros((8, B), np.int64)
            for t in CUTS: l = l + (s >= t)
            u = (16 * x[:, :, None] + ax[q] * s[:, :, None]) >> (4 + l[:, :, None])
            v = (16 * y[:, :, None] + ay[q] * s[:, :, None]) >> (4 + l[:, :, None])
            at = BASE[l][:, :, None] + v * (W >> l)[:, :, None] + u
            e = P[q][g, ch, at.reshape(8, 1, B * K)]
            m = np.max(e.reshape(8, 16, B, NB, Q), axis=4)
            d = np.einsum("gcbn,gcdn->gdb", m.astype(np.int64), H[q]) >> SH
            d = np.minimum(np.maximum(d, -DM), DM)
            s = np.minimum(np.maximum(s + d[:, 2], SMIN), SMAX)
            x = np.minimum(np.maximum(x + d[:, 0], 0), W - s)
            y = np.minimum(np.maximum(y + d[:, 1], 0), W - s)
            trail[r, :, h] = np.stack([x, y, s], axis=1)
        feat[r] = m.transpose(0, 1, 3, 2).reshape(128, NB * B).astype(BF)
    return {"feat": feat, "trail": trail.reshape(N, 8, 3 * N * B)}

@@ -1,0 +1,437 @@
+from concourse.bass import DstId, RemoteDMATransfer
+from concourse.mybir import AluOpType as A, ActivationFunctionType as F
+
+N, C, B = 4, 5440, 128
+PLACE = (0, 1, 2, 0)
+BATCH = (32, 32, 32, 32)
+VCOLS = (16, 20, 20, 16)
+ROUNDS = 1
+TAB_ON_V = 8
+ORDER = """idx0 idx1 first2 first3 conv0 fill1 gv0 conv1 gs0 pool0 idx3 idx2 head0 gv1 gs1 moves0 form0 conv2 conv3 upd0 pool1 head1 gv2 moves1
+form1 gs2 upd1 pool2 gs3 head2 gv3 moves2 form2 pool3 upd2 idx4 head3 conv4 moves3 gv4 fdiag3 gs4 flist3 form3 upd3 idx5 conv5 pool4 gs5 trail0
+head4 gv5 moves4 form4 idx6 pool5 upd4 conv6 head5 moves5 gv6 form5 upd5 idx7 conv7 gs6 gs7 pool6 gv7 head6 moves6 form6 idx8 pool7 head7 upd6
+conv8 moves7 form7 idx9 upd7 gv8 conv9 gs8 gs9 pool8 gv9 head8 moves8 form8 idx10 pool9 upd8 conv10 head9 moves9 form9 gv10 upd9 idx11 conv11
+fhalf3 fcopy3 gs10 trail1 gs11 fhead3 pool10 gv11 head10 moves10 form10 upd10 pool11 idx12 head11 conv12 moves11 form11 idx13 upd11 gv12 conv13
+gs12 gs13 pool12 head12 idx14 gv13 featv12 moves12 conv14 pool13 form12 idx15 head13 gv14 upd12 featv13 conv15 gs14 gs15 feats13 pool14 moves13
+gv15 featv14 form13 head14 pool15 head15 moves14 featv15 upd13 form14 feats12 feats14 feats15 trail2 moves15 upd14 form15 upd15 trail3"""
+SIM = 256
+CUTS = (12, 24, 48)
+BJ = (1.0, -0.5, -0.25, -0.125)
+AJ = (1.0, -0.75, -0.1875, -0.046875)
+KJ = (-127.0 / 256, 4096.0, 1024.0, 256.0)
+NBT = len(BATCH)
+B0 = [sum(BATCH[:b]) for b in range(NBT)]
+FR = [h - PLACE[h] for h in range(N)]
+FAR = sorted(set(f for f in FR if f))
+NH = 6
+PW = -(-C // (8 * NH * ROUNDS)) * 8
+CP = PW * NH * ROUNDS
+
+SCRATCH = {
+    "hd": ("sbuf", [128, 24], "bfloat16"), "sxy": ("sbuf", [128, 4], "int32"), "bx": ("sbuf", [64, 128], "int32"),
+    "ones": ("sbuf", [128, 128], "bfloat16"), "ident": ("sbuf", [128, 128], "bfloat16"),
+    "gcol": ("sbuf", [128, 4, 32], "float32"), "rcol": ("sbuf", [64, 4, 32], "float32"),
+    "pc": ("sbuf", [128, 4], "int32"), "pf": ("sbuf", [128, 4], "float32"),
+    "bd": ("sbuf", [128, 4, 32], "bfloat16"), "mz": ("sbuf", [128, 8], "float32"),
+    "tab": ("sbuf", [128, 5, 4, 32], "bfloat16"),
+    "prs": ("sbuf", [64, 4, 32], "bfloat16"), "prr": ("sbuf", [64, 4, 32], "bfloat16"),
+    "fm": ("sbuf", [64, 3, 4, 32], "bfloat16"), "bias": ("sbuf", [4, 32], "bfloat16"), "lim": ("sbuf", [64, 2], "float32"),
+    "mg": ("sbuf", [128, 256], "bfloat16"), "d1": ("sbuf", [128, 4 * max(BATCH)], "bfloat16"),
+    "is2": ("sbuf", [128, max(BATCH)], "bfloat16"),
+    "pm": ("sbuf", [128, 32 * max(BATCH)], "bfloat16"), "dg": ("sbuf", [128, 512], "bfloat16"),
+    "off": ("sbuf", [128, 1024], "uint16"), "gat": ("sbuf", [128, 16384], "bfloat16"), "pool": ("sbuf", [128, 16384], "bfloat16"),
+    "ee": ("sbuf", [64, 640], "bfloat16"), "fb": ("sbuf", [128, 2, 4, 128], "bfloat16"),
+    "piece": ("sbuf", [128, N * ROUNDS * PW], "bfloat16"),
+    "pi0": ("psum", [128, 512], "float32"), "pi1": ("psum", [128, 512], "float32"),
+    "pz0": ("psum", [128, 512], "float32"), "pz1": ("psum", [128, 512], "float32"),
+    "pt0": ("psum", [128, 512], "float32"), "pt1": ("psum", [128, 512], "float32"),
+    "pu0": ("psum", [128, 512], "float32"), "pu1": ("psum", [128, 512], "float32"),
+}
+for _f in [0] + FAR:
+    SCRATCH["win%d" % _f] = ("sbuf", [128, CP], "bfloat16")
+    SCRATCH["par%d" % _f] = ("sbuf", [128, 28], "float32")
+    SCRATCH["im%d" % _f] = ("sbuf", [128, 512], "bfloat16")
+    SCRATCH["wz%d" % _f] = ("sbuf", [128, 256], "bfloat16")
+for _h in range(N):
+    SCRATCH["ri%d" % _h] = ("sbuf", [128, 512], "bfloat16")
+    SCRATCH["ro%d" % _h] = ("sbuf", [128, 512], "bfloat16")
+    SCRATCH["tb%d" % _h] = ("sbuf", [128, 128], "float32")
+    SCRATCH["tl%d" % _h] = ("sbuf", [128, 128], "float32")
+
+SEMAPHORES = (["cv", "cs", "cp", "cg", "lp", "lh", "lb", "sent", "st"] + ["ap%d" % f for f in FAR] + ["aw%d" % f for f in FAR]
+              + ["ar%d_%d" % (h, b) for h in range(1, N) for b in range(NBT)] + ["at%d" % h for h in range(N)]
+              + ["hp%d_%d" % (f, u) for f in range(N) for u in range(ROUNDS)])
+
+
+def routes(T, topo):
+    out = []
+    for r, c in enumerate(T.cores):
+        mate = [m for m in range(SIM) if topo.mates(c, m)]
+        low = topo.engines(c, T.cores[(r + 1) % N])
+        hs, used, dies = [], [], []
+        high = [e for e in topo.engines(c, [a for a in topo.cores_of(c) if a != c][0]) if e not in low]
+        for a in topo.cores_of(c):
+            if a == c:
+                continue
+            cross = topo.may_write(a, mate[0])
+            if not (cross or topo.die(a) != topo.die(c)):
+                continue
+            relay = None
+            if cross:
+                relay = [m for m in mate if topo.may_write(m, c) and topo.die(m) == topo.die(a) and m not in used][0]
+                used.append(relay)
+            if cross and topo.die(a) not in dies:
+                en = low[4 * len(dies):4 * len(dies) + 4]
+                dies.append(topo.die(a))
+            else:
+                en, high = high[:2], high[2:]
+            hs.append((a, cross, relay, en))
+        out.append(hs)
+    return out
+
+
+def write(g, T, topo, src, dst, out, in_, sem):
+    rid, pid = topo.addr(dst, src)
+    g.remote_dma(out, in_, T.sem[sem], T.sem.sent, pid, rid, topo.mask(src, dst))
+    return len(topo.engines(src, dst))
+
+
+def helper_program(g, core, T, topo):
+    rt = routes(T, topo)
+    sent = 0
+    for r in range(N):
+        for k, (a, cross, relay, en) in enumerate(rt[r]):
+            if a == core:
+                for f in FAR:
+                    d = (r - f) % N
+                    for u in range(ROUNDS):
+                        if f == FAR[0]:
+                            g.wait_ge(T.sem["hp0_%d" % u], len(en))
+                        c0 = (u * NH + k) * PW
+                        src = T.piece[:, u * PW:(u + 1) * PW]
+                        if cross:
+                            s = (f * ROUNDS + u) * PW
+                            sent += write(g, T, topo, core, rt[d][k][2], T.piece[:, s:s + PW], src, "hp%d_%d" % (f, u))
+                        else:
+                            sent += write(g, T, topo, core, T.cores[d], T["win%d" % f][:, c0:c0 + PW], src, "aw%d" % f)
+            if relay == core:
+                for f in FAR:
+                    frm = rt[(r + f) % N][k][0]
+                    for u in range(ROUNDS):
+                        g.wait_ge(T.sem["hp%d_%d" % (f, u)], len(topo.engines(frm, core)))
+                        c0 = (u * NH + k) * PW
+                        s = (f * ROUNDS + u) * PW
+                        sent += write(g, T, topo, core, T.cores[r], T["win%d" % f][:, c0:c0 + PW], T.piece[:, s:s + PW], "aw%d" % f)
+    if sent:
+        g.wait_ge(T.sem.sent, sent)
+
+
+def far_in(h):
+    return h > 0 and PLACE[h] != PLACE[h - 1]
+
+
+def rank_program(g, core, T, topo):
+    rank = T.rank_of(core)
+    if rank is None:
+        helper_program(g, core, T, topo)
+        return
+    V, S, P = g.vector, g.scalar, g.tensor
+    Q = {"v": V, "s": S, "p": P, "g": g, "y": g.sync}
+    cnt = {"v": 0, "s": 0, "p": 0, "g": 0}
+    waited, wr, rd = {}, {}, {}
+    sent = [0]
+    stores = [0]
+
+    def need(q, toks):
+        best = {}
+        for s, n in toks:
+            best[s] = max(best.get(s, 0), n)
+        for s, n in best.items():
+            if waited.get((q, s), 0) < n:
+                Q[q].wait_ge(T.sem[s], n)
+                waited[(q, s)] = n
+
+    def deps(q, R, W):
+        toks = []
+        for k in R:
+            toks += wr.get(k, [])
+        for k in W:
+            toks += wr.get(k, []) + rd.get(k, [])
+        need(q, toks)
+
+    def done(tok, R, W):
+        for k in R:
+            rd.setdefault(k, []).append(tok)
+        for k in W:
+            wr[k] = [tok]
+            rd[k] = []
+
+    def op(q, R, W, *calls):
+        deps(q, R, W)
+        for c in calls:
+            c().then_inc(T.sem["c" + q], 1)
+            cnt[q] += 1
+        done(("c" + q, cnt[q]), R, W)
+
+    def part(q, R, key, *calls):
+        deps(q, R, [])
+        for c in calls:
+            c().then_inc(T.sem["c" + q], 1)
+            cnt[q] += 1
+        wr.setdefault(key, []).append(("c" + q, cnt[q]))
+        done(("c" + q, cnt[q]), R, [])
+
+    def ts(out, in0, s1, o1, s2=None, o2=None):
+        if o2 is None:
+            return lambda: V.tensor_scalar(out, in0, s1, None, o1)
+        return lambda: V.tensor_scalar(out, in0, s1, s2, o1, o2)
+
+    def ms(ap, v):
+        return lambda: V.memset(ap, v)
+
+    def cp(out, in_):
+        return lambda: V.tensor_copy(out, in_)
+
+    def mm(out, l, r, a, z):
+        return lambda: P.matmul(out, l, r, a, z)
+
+    def act(out, in_, scale=None):
+        if scale is None:
+            return lambda: S.activation(out, in_, F.Copy)
+        return lambda: S.activation(out, in_, F.Identity, scale=scale)
+
+    def ramp(out, pattern, base):
+        return lambda: g.iota(out, pattern, base, 0, allow_small_or_imprecise_dtypes=True)
+
+    def send(dst_rank, out, in_, sem, R):
+        deps("g", R, [])
+        sent[0] += write(g, T, topo, core, T.cores[dst_rank % N], out, in_, sem)
+
+    far_inc = len(topo.engines(core, T.cores[(rank + 1) % N]))
+    NM = max(BATCH)
+
+    op("v", [], ["bx"], ms(T.bx[32:64, :], 1))
+    S.dma_start(T.sxy[:, 0:2], T.sx[:]).then_inc(T.sem.lh, 16)
+    S.dma_start(T.sxy[:, 2:4], T.sy[:]).then_inc(T.sem.lh, 16)
+    g.sync.dma_start(T.hd[:], T.head[:]).then_inc(T.sem.lh, 16)
+    deps("y", [], ["bx"])
+    g.sync.dma_start(T.bx[40:64, :], T.box[:]).then_inc(T.sem.lb, 16)
+    g.sync.dma_start(T.win0[:, 0:C], T.pyr[:]).then_inc(T.sem.lp, 16)
+    wr["bx"] = [("lb", 16)]
+    wr["in"] = [("lh", 48)]
+    wr["win0"] = [("lp", 16)]
+    for f in FAR:
+        wr["win%d" % f] = [("aw%d" % f, far_inc * NH * ROUNDS)]
+        wr["par%d" % f] = [("ap%d" % f, far_inc)]
+
+    X_, Y_, S_, O_ = slice(8, 32, 3), slice(9, 32, 3), slice(10, 32, 3), slice(0, 8)
+    fm = T.fm
+    op("g", [], ["pc"], lambda: g.iota(T.pc[:, 0:1], [[0, 1]], 0, 1))
+    op("g", [], ["gcol"], ramp(T.gcol[:, :, 0:8], [[0, 4], [1, 8]], 0), ramp(T.gcol[:, :, 8:32], [[0, 4], [1, 8], [0, 3]], 0))
+    op("v", [], ["ones"], ms(T.ones[:], 1.0))
+    op("v", ["pc"], ["pc2"], ts(T.pc[:, 1:2], T.pc[:, 0:1], 4, A.arith_shift_right), ts(T.pc[:, 2:3], T.pc[:, 0:1], 31, A.bitwise_and))
+    op("v", [], ["tab0"], ms(T.tab[:], 0.0))
+    op("v", ["pc2"], ["pf"], cp(T.pf[:, 0:1], T.pc[:, 1:2]), ts(T.pf[:, 1:2], T.pc[:, 2:3], -10.0, A.add))
+    op("g", [], ["rcol"], ramp(T.rcol[:], [[0, 4], [1, 32]], -10))
+    op("g", ["ones"], ["ident"], lambda: g.affine_select(T.ident[:], T.ones[:], [[-1, 128]], A.is_equal, 0.0, 0, 1))
+    op("v", ["pf", "gcol"], ["bd"], ts(T.bd[:], T.gcol[:], T.pf[:, 0:1], A.is_equal))
+    op("v", ["pf", "gcol"], ["prs"], ts(T.prs[:], T.gcol[0:64], 3.0, A.mult, T.pf[0:64, 1:2], A.is_equal))
+    op("v", ["pf", "rcol"], ["prr"], ts(T.prr[:], T.rcol[:], T.pf[0:64, 1:2], A.is_equal))
+    tabs = []
+    for k, sl, tb in ((4, O_, [1.5 * 2.0 ** 29 * b for b in BJ]), (0, S_, [4 * a for a in AJ]), (2, S_, [b / 16 for b in BJ]), (3, X_, BJ), (3, O_, KJ),
+                      (1, Y_, [64 * a for a in AJ]), (1, O_, [2 * a - 32 * b for a, b in zip(AJ, BJ)])):
+        tabs += [(T.tab[:, k, j, sl], T.bd[:, j, sl], tb[j]) for j in range(4)]
+    part("s", ["bd", "tab0"], "tab", *[act(*t) for t in tabs[TAB_ON_V:]])
+    op("v", ["prs"], ["fm2"], ms(fm[:, 2, 0, :], 0.0), ts(fm[:, 2, 1:4, :], T.prs[:, 1:4, :], 64.0, A.mult))
+    op("v", ["prs", "prr"], ["fm"],
+       ts(fm[:, 0, :, X_], T.prs[:, :, X_], -1.0, A.mult), ts(fm[:, 0, :, Y_], T.prs[:, :, Y_], -1.0, A.mult), cp(fm[:, 0, :, S_], T.prs[:, :, S_]),
+       cp(fm[:, 1, :, X_], T.prr[:, :, X_]), cp(fm[:, 1, :, Y_], T.prr[:, :, Y_]), ms(fm[:, 1, :, S_], 0.0), ms(fm[:, 0:2, :, O_], 0.0))
+    op("g", ["ident"], ["fm2"], ramp(fm[32:33, 2, 0, :], [[0, 32]], 64),
+       *[ramp(fm[32:33, 2, j, :], [[0, 32]], -64 * (191 + CUTS[j - 1])) for j in (1, 2, 3)])
+    op("g", [], ["fm"], ramp(fm[32:33, 0:2], [[-448, 2], [0, 128]], 256))
+    op("g", [], ["fm"], ramp(fm[32:33, 0:2, :, S_], [[256, 2], [0, 32]], -192), ramp(fm[32:33, 1, :, O_], [[0, 32]], 1))
+    op("v", ["bd"], ["mz"], ts(T.mz[:], T.bd[:, 0, 0:8], 1.0 / 512, A.mult))
+    op("v", ["in"], ["par0"], cp(T.par0[:, 24:28], T.sxy[:]), cp(T.par0[:, 0:24], T.hd[:]))
+    part("v", ["bd", "tab0"], "tabv", *[ts(o, i, v, A.mult) for o, i, v in tabs[:TAB_ON_V]])
+    op("p", ["tabv", "ident", "ones"], ["pi1"], mm(T.pi1[:, 0:128], T.tab[:, 4], T.ident[:], True, True),
+       mm(T.pi1[:, 128:128 + NM], T.tab[:, 0], T.ones[:, 0:NM], True, True))
+    wr["tab"] = wr["tab"] + wr["tabv"]
+    op("v", [], ["d1"], ms(T.d1[:], 0.0))
+    op("v", ["bx"], ["ee-1"], ms(T.ee[0:32, 512:640], 192.0), cp(T.ee[32:64, 512:640], T.bx[32:64, :]))
+    op("v", [], ["pi1", "is2", "mg"], ts(T.is2[:], T.pi1[:, 128:128 + NM], 0.0, A.not_equal, -4.0, A.mult),
+       cp(T.mg[:, 0:128], T.pi1[:, 0:128]), ts(T.mg[:, 128:256], T.pi1[:, 0:128], -1.0, A.mult))
+    op("v", ["is2"], ["d1"], ts(T.d1[:, 0::4], T.is2[:], 60.0, A.add), ts(T.d1[:, 1::4], T.is2[:], 8.0, A.add))
+    op("v", [], ["pad"], ms(T.win0[:, C:CP], 0.0))
+
+    for f in FAR:
+        send(rank - f, T["par%d" % f][:], T.par0[:], "ap%d" % f, ["par0"])
+
+    def frame_diag(f):
+        par = T["par%d" % f]
+        op("s", ["par%d" % f, "ident"], ["dg"], *[act(T.dg[:, 128 * k:128 * k + 128], T.ident[:], par[:, 24 + k:25 + k]) for k in range(4)])
+
+    def frame_lists(f):
+        op("p", ["dg", "tab", "ident"], ["pu0"],
+           *[mm(T.pu0[:, 128 * k:128 * k + 128], T.tab[:, (2 if k < 2 else 0) + i], (T.dg[:, 128 * k:128 * k + 128] if i == 0 else T.ident[:]),
+                i == 0, i == 1) for k in range(4) for i in range(2)])
+
+    def frame_copy(f):
+        op("s", [], ["pu0", "im%d" % f], act(T["im%d" % f][:], T.pu0[:]))
+
+    def frame_head(f, ks):
+        par, wz = T["par%d" % f], T["wz%d" % f]
+        part("s", ["par%d" % f, "mz"], "wz%d" % f, *[act(wz[:, 64 + 24 * k:88 + 24 * k], par[:, 0:24], T.mz[:, k:k + 1]) for k in ks])
+
+    def forms(bank, e, n, R, fresh):
+        op("p", R + ["fm", "fm2"], [bank], *[mm(T[bank][:, k:4 * n:4], fm[:, (k + 2) % 3], e, True, True) for k in range(0 if fresh else 1, 4)])
+
+    def update(bank, c0, out, n, key, W):
+        op("v", ["d1"], W + [key], lambda: V.tensor_tensor_scan(out, T[bank][:, c0:c0 + 4 * n], T.d1[:, 0:4 * n], 0.0, A.min, A.max))
+
+    def first(b):
+        lo, hi = 4 * B0[b], 4 * (B0[b] + BATCH[b])
+        need("v", formed)
+        update("pu1", lo, T.ri0[:, lo:hi], BATCH[b], ("ri", 0, b), [])
+
+    def fills(i):
+        if i == 0:
+            op("v", [], ["bias"], ms(T.bias[0:3, 8:32], 2.0 ** -10), ms(T.bias[0:3, 0:8], 0.0))
+            part("v", [], "pm", ms(T.pm[:, 0::4], 0.0), ms(T.pm[:, 1::4], 256.0))
+            op("v", [], ["bias"], ms(T.bias[0:2, 8:32], -0.5))
+            part("v", [], "wz0", ms(T.wz0[:, 0:64], 0.0))
+            op("v", [], ["bias"], ms(T.bias[0:1, 8:32], 192.0))
+        else:
+            part("v", [], "pm", ms(T.pm[:, 2::4], 256.0), ms(T.pm[:, 3::4], 256.0))
+            op("v", [], ["lim"], ms(T.lim[0:32, 0:1], 180.0), ms(T.lim[32:64, 0:1], 0.0), ms(T.lim[0:32, 1:2], 204.0), ms(T.lim[32:64, 1:2], 255.0))
+            for f in FAR:
+                part("v", [], "wz%d" % f, ms(T["wz%d" % f][:, 0:64], 0.0))
+
+    frame_diag(0)
+    frame_lists(0)
+    forms("pu1", T.ee[:, 512:640], B, ["ee-1"], True)
+    formed = wr["pu1"]
+    frame_head(0, range(4))
+    frame_copy(0)
+    frame_head(0, range(4, 8))
+    first(0)
+    first(1)
+    fills(0)
+
+    deps("g", ["win0", "pad"], [])
+    for u in range(ROUNDS):
+        tr = []
+        for k, (a, cross, relay, en) in enumerate(routes(T, topo)[rank]):
+            rid, pid = topo.addr(a, core)
+            c0 = (u * NH + k) * PW
+            tr.append(RemoteDMATransfer(dst_ids=[DstId(rid=rid, pnc=pid)], dma_engine_mask=sum(1 << e for e in en),
+                                        remote_sem=T.sem["hp0_%d" % u], src=T.win0[:, c0:c0 + PW], dst=T.piece[:, u * PW:(u + 1) * PW]))
+            sent[0] += len(en)
+        g.remote_dma_fused(tr, local_sem=T.sem.sent)
+
+    def rin(s):
+        h, b = divmod(s, NBT)
+        buf = T["ri%d" % h] if (h == 0 or far_in(h)) else T["ro%d" % (h - 1)]
+        key = ("ri", h, b) if (h == 0 or far_in(h)) else ("ro", h - 1, b)
+        return buf, 4 * B0[b] + 3, 4 * (B0[b] + BATCH[b]), key
+
+    for h in range(1, N):
+        if far_in(h):
+            for b in range(NBT):
+                wr[("ri", h, b)] = [("ar%d_%d" % (h, b), far_inc)]
+
+    def geo(s):
+        h, b = divmod(s, NBT)
+        return h, b, BATCH[b], 2 * (B * h + B0[b])
+
+    def idx(s):
+        h, b, n, c = geo(s)
+        buf, lo, hi, key = rin(s)
+        r, im, bank = buf[:, lo:hi:4], T["im%d" % FR[h]], "pi%d" % (s % 2)
+        calls = []
+        for k in range(2):
+            o = T[bank][:, k * n:(k + 1) * n]
+            calls += [mm(o, im[:, 256 + 128 * k:384 + 128 * k], r, True, False), mm(o, T.mg[:, 0:128], r, False, False),
+                      mm(o, T.mg[:, 128:256], r, False, False), mm(o, im[:, 128 * k:128 * k + 128], r, False, True)]
+        op("p", [key, "im%d" % FR[h], "mg"], [bank], *calls)
+
+    def gather(s, q):
+        h, b, n, c = geo(s)
+        k = VCOLS[h] * n // 64 * 2
+        lo, hi = (c, c + k) if q == "v" else (c + k, c + 2 * n)
+        src = T["win%d" % FR[h]][:, 0:C].indirect(T.off[:, lo:hi])
+        part(q, [("off", s), "win%d" % FR[h]], ("gat", s), (cp if q == "v" else act)(T.gat[:, 16 * lo:16 * hi], src))
+
+    def conv(s):
+        h, b, n, c = geo(s)
+        bank = "pi%d" % (s % 2)
+        op("v", [], [bank, ("off", s)], ts(T.off[:, c:c + 2 * n], T[bank][:, 0:2 * n], 1.5 * 2.0 ** 23, A.add, 1.5 * 2.0 ** 23, A.subtract))
+
+    def pool(s):
+        h, b, n, c = geo(s)
+        op("v", [("gat", s), "pm"], [("pool", s)],
+           lambda: V.tensor_tensor_scan(T.pool[:, 16 * c:16 * c + 32 * n], T.pm[:, 0:32 * n], T.gat[:, 16 * c:16 * c + 32 * n], 0.0, A.min, A.max))
+
+    def head(s):
+        h, b, n, c = geo(s)
+        buf, lo, hi, key = rin(s)
+        bank, wz = "pz%d" % (s % 2), T["wz%d" % FR[h]]
+        op("p", [key, "prr", "bias"], [bank], mm(T[bank][32:64, 0:n], T.prr[0:32, 0], buf[0:32, lo:hi:4], True, True),
+           mm(T[bank][0:32, 0:n], T.bias[0:3, :], buf[0:3, lo:hi:4], True, False))
+        calls = []
+        for m in range(8):
+            a = 16 * (c + (m // 4) * n) + 4 * (m % 4) + 3
+            calls.append(mm(T[bank][0:32, 0:n], wz[:, m::8], T.pool[:, a:a + 16 * (n - 1) + 1:16], False, m == 7))
+        wr.pop(bank)
+        op("p", [("pool", s), "wz%d" % FR[h]], [bank], *calls)
+
+    def moves(s):
+        h, b, n, c = geo(s)
+        bank = "pz%d" % (s % 2)
+        op("v", ["lim"], [bank, ("ee", s)], ts(T.ee[:, c // 2:c // 2 + n], T[bank][0:64, 0:n], T.lim[:, 0:1], A.max, T.lim[:, 1:2], A.min))
+
+    def form(s):
+        h, b, n, c = geo(s)
+        forms("pt%d" % (s % 2), T.ee[:, c // 2:c // 2 + n], n, [("ee", s)], s < 2)
+
+    def upd(s):
+        h, b, n, c = geo(s)
+        lo, hi = 4 * B0[b], 4 * (B0[b] + n)
+        update("pt%d" % (s % 2), 0, T["ro%d" % h][:, lo:hi], n, ("ro", h, b), ["pt%d" % (s % 2)])
+        if h + 1 < N and far_in(h + 1):
+            send(rank - PLACE[h] + PLACE[h + 1], T["ri%d" % (h + 1)][:, lo:hi], T["ro%d" % h][:, lo:hi], "ar%d_%d" % (h + 1, b), [("ro", h, b)])
+
+    def store(out, in_, R):
+        deps("y", R, [])
+        g.sync.dma_start(out, in_).then_inc(T.sem.st, 16)
+        stores[0] += 16
+
+    def feats(s, q):
+        h, b, n, c = geo(s)
+        part(q, [("pool", s)], "fb", *[(cp if q == "v" else act)(T.fb[:, :, m, B0[b]:B0[b] + n], T.pool[:, 16 * c + 4 * m + 3:16 * c + 32 * n:16])
+                                       for m in ((0, 1) if q == "v" else (2, 3))])
+        if len(wr["fb"]) == 2 * NBT:
+            store(T.feat[:], T.fb[:], ["fb"])
+
+    def trail(h):
+        q = "v" if h == N - 1 else "s"
+        name = "ri" if PLACE[h] and PLACE[h + 1] == 0 else "ro"
+        k = h + 1 if name == "ri" else h
+        op(q, [(name, k, b) for b in range(NBT)], [("tb", h)], (cp if q == "v" else act)(T["tb%d" % h][:], T["%s%d" % (name, k)][:, 3::4]))
+        if PLACE[h] and PLACE[h + 1]:
+            send(rank - PLACE[h], T["tl%d" % h][:], T["tb%d" % h][:], "at%d" % h, [("tb", h)])
+            wr[("tl", h)] = [("at%d" % h, far_inc)]
+            store(T.trail[:, 384 * h:384 * h + 384], T["tl%d" % h][8:32, :], [("tl", h)])
+        else:
+            store(T.trail[:, 384 * h:384 * h + 384], T["tb%d" % h][8:32, :], [("tb", h)])
+
+    steps = {"idx": idx, "conv": conv, "gv": lambda s: gather(s, "v"), "gs": lambda s: gather(s, "s"), "pool": pool, "head": head,
+             "moves": moves, "form": form, "upd": upd, "first": first, "fill": fills, "trail": trail,
+             "featv": lambda s: feats(s, "v"), "feats": lambda s: feats(s, "s"), "fdiag": frame_diag, "flist": frame_lists,
+             "fcopy": frame_copy, "fhalf": lambda f: frame_head(f, range(4)), "fhead": lambda f: frame_head(f, range(4, 8))}
+    for word in ORDER.split():
+        name = word.rstrip("0123456789")
+        steps[name](int(word[len(name):]))
+
+    g.sync.wait_ge(T.sem.st, stores[0])
+    need("y", [("c" + q, cnt[q]) for q in "vspg"])
+    g.wait_ge(T.sem.sent, sent[0])

@@ -2,18 +2,19 @@ from concourse.bass import DstId, RemoteDMATransfer
 from concourse.mybir import AluOpType as A, ActivationFunctionType as F
 
 N, C, B = 4, 5440, 128
-PLACE = (0, 1, 2, 0)
+PLACE = (0, 1, 0, 0)
 BATCH = (32, 32, 32, 32)
-VCOLS = (16, 20, 20, 16)
-ROUNDS = 1
+VCOLS = (16, 20, 16, 14)
+ROUNDS = 2
 TAB_ON_V = 8
-ORDER = """idx0 idx1 first2 first3 conv0 fill1 gv0 conv1 gs0 pool0 idx3 idx2 head0 gv1 gs1 moves0 form0 conv2 conv3 upd0 pool1 head1 gv2 moves1
-form1 gs2 upd1 pool2 gs3 head2 gv3 moves2 form2 pool3 upd2 idx4 head3 conv4 moves3 gv4 fdiag3 gs4 flist3 form3 upd3 idx5 conv5 pool4 gs5 trail0
-head4 gv5 moves4 form4 idx6 pool5 upd4 conv6 head5 moves5 gv6 form5 upd5 idx7 conv7 gs6 gs7 pool6 gv7 head6 moves6 form6 idx8 pool7 head7 upd6
-conv8 moves7 form7 idx9 upd7 gv8 conv9 gs8 gs9 pool8 gv9 head8 moves8 form8 idx10 pool9 upd8 conv10 head9 moves9 form9 gv10 upd9 idx11 conv11
-fhalf3 fcopy3 gs10 trail1 gs11 fhead3 pool10 gv11 head10 moves10 form10 upd10 pool11 idx12 head11 conv12 moves11 form11 idx13 upd11 gv12 conv13
-gs12 gs13 pool12 head12 idx14 gv13 featv12 moves12 conv14 pool13 form12 idx15 head13 gv14 upd12 featv13 conv15 gs14 gs15 feats13 pool14 moves13
-gv15 featv14 form13 head14 pool15 head15 moves14 featv15 upd13 form14 feats12 feats14 feats15 trail2 moves15 upd14 form15 upd15 trail3"""
+ORDER = """fwd0 fwd1 idx0 first2 first3 conv0 idx1 idx2 gs0 fill1 gv0 conv2 conv1 pool0 gv2 head0 idx3 moves0 form0 gs2 gs1 gv1 upd0 conv3 pool2 pool1
+gv3 gs3 fdiag2 fhalf2 head1 head2 moves1 form1 moves2 upd1 form2 upd2 pool3 idx4 head3 conv4 moves3 form3 flist2 gv4 upd3 gs4 trail0 fcopy2
+fhead2 idx5 pool4 head4 conv5 moves4 idx6 form4 gv5 upd4 conv6 gs5 gs6 pool5 gv6 head5 moves5 form5 idx7 pool6 conv7 upd5 head6 gv7 moves6
+fhalf3 fdiag3 form6 flist3 upd6 gs7 pool7 idx8 head7 conv8 moves7 form7 idx9 upd7 gv8 conv9 fhead3 fcopy3 gs8 gs9 pool8 idx10 head8 gv9 conv10
+gv10 moves8 gs10 form8 idx11 pool9 upd8 head9 idx12 conv11 pool10 moves9 gv11 conv12 gs11 form9 head10 upd9 moves10 pool11 idx13 form10 head11
+gs12 upd10 gv12 conv13 moves11 gs13 idx14 form11 pool12 head12 upd11 gv13 idx15 conv14 moves12 conv15 gv14 gv15 pool13 gs14 pool14 featv12
+featv13 form12 head13 moves13 head14 upd12 featv14 moves14 form13 gs15 pool15 upd13 head15 form14 featv15 trail1 feats12 feats14 feats13 feats15
+trail2 moves15 form15 upd14 upd15 trail3"""
 SIM = 256
 CUTS = (12, 24, 48)
 BJ = (1.0, -0.5, -0.25, -0.125)
@@ -26,37 +27,24 @@ FAR = sorted(set(f for f in FR if f))
 NH = 6
 PW = -(-C // (8 * NH * ROUNDS)) * 8
 CP = PW * NH * ROUNDS
+NM = max(BATCH)
+BF, F32 = "bfloat16", "float32"
 
-SCRATCH = {
-    "hd": ("sbuf", [128, 24], "bfloat16"), "sxy": ("sbuf", [128, 4], "int32"), "bx": ("sbuf", [64, 128], "int32"),
-    "ones": ("sbuf", [128, 128], "bfloat16"), "ident": ("sbuf", [128, 128], "bfloat16"),
-    "gcol": ("sbuf", [128, 4, 32], "float32"), "rcol": ("sbuf", [64, 4, 32], "float32"),
-    "pc": ("sbuf", [128, 4], "int32"), "pf": ("sbuf", [128, 4], "float32"),
-    "bd": ("sbuf", [128, 4, 32], "bfloat16"), "mz": ("sbuf", [128, 8], "float32"),
-    "tab": ("sbuf", [128, 5, 4, 32], "bfloat16"),
-    "prs": ("sbuf", [64, 4, 32], "bfloat16"), "prr": ("sbuf", [64, 4, 32], "bfloat16"),
-    "fm": ("sbuf", [64, 3, 4, 32], "bfloat16"), "bias": ("sbuf", [4, 32], "bfloat16"), "lim": ("sbuf", [64, 2], "float32"),
-    "mg": ("sbuf", [128, 256], "bfloat16"), "d1": ("sbuf", [128, 4 * max(BATCH)], "bfloat16"),
-    "is2": ("sbuf", [128, max(BATCH)], "bfloat16"),
-    "pm": ("sbuf", [128, 32 * max(BATCH)], "bfloat16"), "dg": ("sbuf", [128, 512], "bfloat16"),
-    "off": ("sbuf", [128, 1024], "uint16"), "gat": ("sbuf", [128, 16384], "bfloat16"), "pool": ("sbuf", [128, 16384], "bfloat16"),
-    "ee": ("sbuf", [64, 640], "bfloat16"), "fb": ("sbuf", [128, 2, 4, 128], "bfloat16"),
-    "piece": ("sbuf", [128, N * ROUNDS * PW], "bfloat16"),
-    "pi0": ("psum", [128, 512], "float32"), "pi1": ("psum", [128, 512], "float32"),
-    "pz0": ("psum", [128, 512], "float32"), "pz1": ("psum", [128, 512], "float32"),
-    "pt0": ("psum", [128, 512], "float32"), "pt1": ("psum", [128, 512], "float32"),
-    "pu0": ("psum", [128, 512], "float32"), "pu1": ("psum", [128, 512], "float32"),
-}
+SCRATCH = {k: ("sbuf", s, d) for k, s, d in (
+    ("hd", [128, 24], BF), ("sxy", [128, 4], "int32"), ("bx", [64, 128], "int32"), ("ones", [128, 128], BF), ("ident", [128, 128], BF),
+    ("gcol", [128, 4, 32], F32), ("rcol", [64, 4, 32], F32), ("pc", [128, 4], "int32"), ("pf", [128, 4], F32), ("bd", [128, 4, 32], BF),
+    ("mz", [128, 8], F32), ("tab", [128, 5, 4, 32], BF), ("prs", [64, 4, 32], BF), ("prr", [64, 4, 32], BF), ("fm", [64, 3, 4, 32], BF),
+    ("bias", [4, 32], BF), ("lim", [64, 2], F32), ("mg", [128, 256], BF), ("d1", [128, 4 * NM], BF), ("is2", [128, NM], BF),
+    ("pm", [128, 32 * NM], BF), ("dg", [128, 512], BF), ("off", [128, 1024], "uint16"), ("gat", [128, 16384], BF), ("pool", [128, 16384], BF),
+    ("ee", [64, 640], BF), ("fb", [128, 2, 4, 128], BF), ("piece", [128, N * ROUNDS * PW], BF))}
+for _k in ("pi0", "pi1", "pz0", "pz1", "pt0", "pt1", "pu0", "pu1"):
+    SCRATCH[_k] = ("psum", [128, 512], F32)
 for _f in [0] + FAR:
-    SCRATCH["win%d" % _f] = ("sbuf", [128, CP], "bfloat16")
-    SCRATCH["par%d" % _f] = ("sbuf", [128, 28], "float32")
-    SCRATCH["im%d" % _f] = ("sbuf", [128, 512], "bfloat16")
-    SCRATCH["wz%d" % _f] = ("sbuf", [128, 256], "bfloat16")
+    for _k, _w, _d in (("win", CP, BF), ("par", 28, F32), ("im", 512, BF), ("wz", 256, BF)):
+        SCRATCH["%s%d" % (_k, _f)] = ("sbuf", [128, _w], _d)
 for _h in range(N):
-    SCRATCH["ri%d" % _h] = ("sbuf", [128, 512], "bfloat16")
-    SCRATCH["ro%d" % _h] = ("sbuf", [128, 512], "bfloat16")
-    SCRATCH["tb%d" % _h] = ("sbuf", [128, 128], "float32")
-    SCRATCH["tl%d" % _h] = ("sbuf", [128, 128], "float32")
+    for _k, _w, _d in (("ri", 512, BF), ("ro", 512, BF), ("tb", 128, F32), ("tl", 128, F32)):
+        SCRATCH["%s%d" % (_k, _h)] = ("sbuf", [128, _w], _d)
 
 SEMAPHORES = (["cv", "cs", "cp", "cg", "lp", "lh", "lb", "sent", "st"] + ["ap%d" % f for f in FAR] + ["aw%d" % f for f in FAR]
               + ["ar%d_%d" % (h, b) for h in range(1, N) for b in range(NBT)] + ["at%d" % h for h in range(N)]
@@ -174,12 +162,8 @@ def rank_program(g, core, T, topo):
         done(("c" + q, cnt[q]), R, W)
 
     def part(q, R, key, *calls):
-        deps(q, R, [])
-        for c in calls:
-            c().then_inc(T.sem["c" + q], 1)
-            cnt[q] += 1
+        op(q, R, [], *calls)
         wr.setdefault(key, []).append(("c" + q, cnt[q]))
-        done(("c" + q, cnt[q]), R, [])
 
     def ts(out, in0, s1, o1, s2=None, o2=None):
         if o2 is None:
@@ -208,7 +192,6 @@ def rank_program(g, core, T, topo):
         sent[0] += write(g, T, topo, core, T.cores[dst_rank % N], out, in_, sem)
 
     far_inc = len(topo.engines(core, T.cores[(rank + 1) % N]))
-    NM = max(BATCH)
 
     op("v", [], ["bx"], ms(T.bx[32:64, :], 1))
     S.dma_start(T.sxy[:, 0:2], T.sx[:]).then_inc(T.sem.lh, 16)
@@ -317,8 +300,8 @@ def rank_program(g, core, T, topo):
     first(1)
     fills(0)
 
-    deps("g", ["win0", "pad"], [])
-    for u in range(ROUNDS):
+    def fwd(u):
+        deps("g", ["win0", "pad"], [])
         tr = []
         for k, (a, cross, relay, en) in enumerate(routes(T, topo)[rank]):
             rid, pid = topo.addr(a, core)
@@ -425,7 +408,7 @@ def rank_program(g, core, T, topo):
             store(T.trail[:, 384 * h:384 * h + 384], T["tb%d" % h][8:32, :], [("tb", h)])
 
     steps = {"idx": idx, "conv": conv, "gv": lambda s: gather(s, "v"), "gs": lambda s: gather(s, "s"), "pool": pool, "head": head,
-             "moves": moves, "form": form, "upd": upd, "first": first, "fill": fills, "trail": trail,
+             "moves": moves, "form": form, "upd": upd, "first": first, "fill": fills, "trail": trail, "fwd": fwd,
              "featv": lambda s: feats(s, "v"), "feats": lambda s: feats(s, "s"), "fdiag": frame_diag, "flist": frame_lists,
              "fcopy": frame_copy, "fhalf": lambda f: frame_head(f, range(4)), "fhead": lambda f: frame_head(f, range(4, 8))}
     for word in ORDER.split():

@@ -3,119 +3,133 @@ from concourse.mybir import AluOpType as A, ActivationFunctionType as F
 
 N, C, B = 4, 5440, 128
 PLACE = (0, 1, 0, 0)
-BATCH = (32, 32, 32, 32)
-VCOLS = (16, 20, 16, 14)
-ROUNDS = 2
-TAB_ON_V = 8
-ORDER = """fwd0 fwd1 idx0 first2 first3 conv0 idx1 idx2 gs0 fill1 gv0 conv2 conv1 pool0 gv2 head0 idx3 moves0 form0 gs2 gs1 gv1 upd0 conv3 pool2 pool1
-gv3 gs3 fdiag2 fhalf2 head1 head2 moves1 form1 moves2 upd1 form2 upd2 pool3 idx4 head3 conv4 moves3 form3 flist2 gv4 upd3 gs4 trail0 fcopy2
-fhead2 idx5 pool4 head4 conv5 moves4 idx6 form4 gv5 upd4 conv6 gs5 gs6 pool5 gv6 head5 moves5 form5 idx7 pool6 conv7 upd5 head6 gv7 moves6
-fhalf3 fdiag3 form6 flist3 upd6 gs7 pool7 idx8 head7 conv8 moves7 form7 idx9 upd7 gv8 conv9 fhead3 fcopy3 gs8 gs9 pool8 idx10 head8 gv9 conv10
-gv10 moves8 gs10 form8 idx11 pool9 upd8 head9 idx12 conv11 pool10 moves9 gv11 conv12 gs11 form9 head10 upd9 moves10 pool11 idx13 form10 head11
-gs12 upd10 gv12 conv13 moves11 gs13 idx14 form11 pool12 head12 upd11 gv13 idx15 conv14 moves12 conv15 gv14 gv15 pool13 gs14 pool14 featv12
-featv13 form12 head13 moves13 head14 upd12 featv14 moves14 form13 gs15 pool15 upd13 head15 form14 featv15 trail1 feats12 feats14 feats13 feats15
-trail2 moves15 form15 upd14 upd15 trail3"""
+BATCH = ((32, 32, 32, 32), (32, 32, 32, 32), (32, 32, 32, 32), (32, 32, 32, 32))
+VCOLS = (16, 16, 18, 16)
+VFIRST = (28, 22, 26, 18)
+LAST = (0, 0, 0, 0)
+VTWO = (0, 0, 0, 0)
+GAP = (0.4, 0.4, 0.0)
+LEAD = (1.0, 0.5, -0.45, -0.7, 0.4, 0.15, -0.45, -0.7, 0.4, 0.15, -0.65, -0.65, 0.85, 0.45, -0.65, -0.65)
+LAG = (-0.15, 0.45, 0.65, 0.7, 0.95, 0.0, 0.9, 0.65, 0.7, 1.1, 0, 0.45, 0.8, 0.9, 1.3, 0, 0.45, 0.8, 0.9, 1.3)
+FEAT_G = 3
+PLAN = (("wz", 128, "b0 b1", "hi", (2, 3), 0), ("im", 128, "m0 m1 m2 m3", "all", (2, 3), 0), ("win", 640, "m0 m2", "lo", (2, 3), 0), ("win", 720, "m1 m3", "hi", (2, 3), 0), ("win", 720, "b0 b1", "hi", (2, 3), 0), ("win", 480, "", "lo", (), 0), ("win", 800, "", "lo", (), 0))
+DIRECT = ((2, 2, 5), (4, 2, 6), (6, 3, 5), (8, 3, 6))
+SUB = 3
+AENG = 2
+PM_G = 384
+FIRST_AT = 1.2
 SIM = 256
 CUTS = (12, 24, 48)
 BJ = (1.0, -0.5, -0.25, -0.125)
 AJ = (1.0, -0.75, -0.1875, -0.046875)
 KJ = (-127.0 / 256, 4096.0, 1024.0, 256.0)
-NBT = len(BATCH)
-B0 = [sum(BATCH[:b]) for b in range(NBT)]
+B0 = [[sum(bs[:b]) for b in range(len(bs))] for bs in BATCH]
+STEP = [(h, b) for h in range(N) for b in range(len(BATCH[h]))]
 FR = [h - PLACE[h] for h in range(N)]
 FAR = sorted(set(f for f in FR if f))
-NH = 6
-PW = -(-C // (8 * NH * ROUNDS)) * 8
-CP = PW * NH * ROUNDS
-NM = max(BATCH)
+NM = max(max(bs) for bs in BATCH)
 BF, F32 = "bfloat16", "float32"
+
+PIECES, SPAN, WIDE = {}, [], {}
+for _i, (_b, _w, _names, _pool, _fs, _when) in enumerate(PLAN):
+    SPAN.append((_b, WIDE.get(_b, 0), WIDE.get(_b, 0) + _w * max(len(_names.split()), 1)))
+    for _j, _k in enumerate(_names.split()):
+        PIECES.setdefault(_k, []).append((_i, _b, SPAN[_i][1] + _j * _w, _w, sum(p[3] for p in PIECES.get(_k, [])), _fs))
+    WIDE[_b] = SPAN[_i][2]
+CP = WIDE["win"]
+PT = max(sum(p[3] for p in ps) for ps in PIECES.values())
+PN = max(len(ps) for ps in PIECES.values())
 
 SCRATCH = {k: ("sbuf", s, d) for k, s, d in (
     ("hd", [128, 24], BF), ("sxy", [128, 4], "int32"), ("bx", [64, 128], "int32"), ("ones", [128, 128], BF), ("ident", [128, 128], BF),
-    ("gcol", [128, 4, 32], F32), ("rcol", [64, 4, 32], F32), ("pc", [128, 4], "int32"), ("pf", [128, 4], F32), ("bd", [128, 4, 32], BF),
-    ("mz", [128, 8], F32), ("tab", [128, 5, 4, 32], BF), ("prs", [64, 4, 32], BF), ("prr", [64, 4, 32], BF), ("fm", [64, 3, 4, 32], BF),
-    ("bias", [4, 32], BF), ("lim", [64, 2], F32), ("mg", [128, 256], BF), ("d1", [128, 4 * NM], BF), ("is2", [128, NM], BF),
+    ("gcol", [128, 4, 32], F32), ("pc", [128, 4], F32), ("pf", [128, 4], F32), ("bd", [128, 2, 8], BF),
+    ("mz", [128, 8], F32), ("tab", [128, 5, 132], BF), ("fm", [65, 3, 4, 32], BF),
+    ("bias", [4, 32], BF), ("lim", [64, 2], F32), ("mg", [128, 256], BF), ("d1", [128, 4 * NM], BF), ("par", [128, 4], F32),
     ("pm", [128, 32 * NM], BF), ("dg", [128, 512], BF), ("off", [128, 1024], "uint16"), ("gat", [128, 16384], BF), ("pool", [128, 16384], BF),
-    ("ee", [64, 640], BF), ("fb", [128, 2, 4, 128], BF), ("piece", [128, N * ROUNDS * PW], BF))}
+    ("ee", [65, 128], BF), ("fb", [128, 2, 4, 128], BF), ("piece", [128, len(FAR) * PT], BF))}
 for _k in ("pi0", "pi1", "pz0", "pz1", "pt0", "pt1", "pu0", "pu1"):
     SCRATCH[_k] = ("psum", [128, 512], F32)
 for _f in [0] + FAR:
-    for _k, _w, _d in (("win", CP, BF), ("par", 28, F32), ("im", 512, BF), ("wz", 256, BF)):
-        SCRATCH["%s%d" % (_k, _f)] = ("sbuf", [128, _w], _d)
+    for _k, _w in (("win", CP), ("im", 512), ("wz", 256)):
+        SCRATCH["%s%d" % (_k, _f)] = ("sbuf", [128, _w], BF)
 for _h in range(N):
-    for _k, _w, _d in (("ri", 512, BF), ("ro", 512, BF), ("tb", 128, F32), ("tl", 128, F32)):
+    for _k, _w, _d in (("ri", 512, BF), ("ro", 512, BF), ("tb", 128, F32)):
         SCRATCH["%s%d" % (_k, _h)] = ("sbuf", [128, _w], _d)
 
-SEMAPHORES = (["cv", "cs", "cp", "cg", "lp", "lh", "lb", "sent", "st"] + ["ap%d" % f for f in FAR] + ["aw%d" % f for f in FAR]
-              + ["ar%d_%d" % (h, b) for h in range(1, N) for b in range(NBT)] + ["at%d" % h for h in range(N)]
-              + ["hp%d_%d" % (f, u) for f in range(N) for u in range(ROUNDS)])
+SEMAPHORES = (["cv", "cs", "cp", "cg", "lp", "lh", "ls", "lb", "sent", "st"] + ["%s%d" % (k, f) for k in WIDE for f in FAR]
+              + ["ar%d_%d" % hb for hb in STEP] + ["hp%d" % j for j in range(PN)]
+              + ["hr%d_%d_%d" % (f, j, u) for f in FAR for j in range(PN) for u in range(SUB)])
 
 
 def routes(T, topo):
     out = []
-    for r, c in enumerate(T.cores):
+    for c in T.cores:
         mate = [m for m in range(SIM) if topo.mates(c, m)]
-        low = topo.engines(c, T.cores[(r + 1) % N])
-        hs, used, dies = [], [], []
-        high = [e for e in topo.engines(c, [a for a in topo.cores_of(c) if a != c][0]) if e not in low]
-        for a in topo.cores_of(c):
-            if a == c:
-                continue
-            cross = topo.may_write(a, mate[0])
-            if not (cross or topo.die(a) != topo.die(c)):
-                continue
-            relay = None
-            if cross:
-                relay = [m for m in mate if topo.may_write(m, c) and topo.die(m) == topo.die(a) and m not in used][0]
-                used.append(relay)
-            if cross and topo.die(a) not in dies:
-                en = low[4 * len(dies):4 * len(dies) + 4]
-                dies.append(topo.die(a))
-            else:
-                en, high = high[:2], high[2:]
-            hs.append((a, cross, relay, en))
+        rest = sorted((a for a in topo.cores_of(c) if a != c), key=lambda a: topo.die(a) != topo.die(c))
+        cross = [a for a in rest if topo.may_write(a, mate[0])]
+        relay = sorted((m for m in mate if topo.may_write(m, c)), key=lambda m: topo.die(m) != topo.die(c))
+        hs = {"m%d" % i: (a, relay[i]) for i, a in enumerate(cross)}
+        for name, same in (("a", True), ("b", False)):
+            hs.update({"%s%d" % (name, i): (a, None)
+                       for i, a in enumerate(a for a in rest if a not in cross and (topo.die(a) == topo.die(c)) == same)})
         out.append(hs)
     return out
 
 
-def write(g, T, topo, src, dst, out, in_, sem):
+def feeds(T, topo, r, i):
+    c, names = T.cores[r], PLAN[i][2].split()
+    low = topo.engines(c, T.cores[(r + 1) % N])
+    every = topo.engines(c, routes(T, topo)[r]["a0"][0])
+    pool = {"lo": low, "hi": [e for e in every if e not in low], "all": every}[PLAN[i][3]]
+    m = len(pool) // len(names)
+    return [(k, pool[m * j:m * j + m]) for j, k in enumerate(names)]
+
+
+def write(g, T, topo, src, dst, out, in_, sem, most=None):
     rid, pid = topo.addr(dst, src)
-    g.remote_dma(out, in_, T.sem[sem], T.sem.sent, pid, rid, topo.mask(src, dst))
-    return len(topo.engines(src, dst))
+    en = topo.engines(src, dst)[:most]
+    g.remote_dma(out, in_, T.sem[sem], T.sem.sent, pid, rid, sum(1 << e for e in en))
+    return len(en)
+
+
+def parts(b, w):
+    n = SUB if b == "win" else 1
+    cut = [8 * ((w // 8) * u // n) for u in range(n + 1)]
+    return list(enumerate(zip(cut, cut[1:])))
 
 
 def helper_program(g, core, T, topo):
     rt = routes(T, topo)
     sent = 0
     for r in range(N):
-        for k, (a, cross, relay, en) in enumerate(rt[r]):
-            if a == core:
-                for f in FAR:
-                    d = (r - f) % N
-                    for u in range(ROUNDS):
-                        if f == FAR[0]:
-                            g.wait_ge(T.sem["hp0_%d" % u], len(en))
-                        c0 = (u * NH + k) * PW
-                        src = T.piece[:, u * PW:(u + 1) * PW]
-                        if cross:
-                            s = (f * ROUNDS + u) * PW
-                            sent += write(g, T, topo, core, rt[d][k][2], T.piece[:, s:s + PW], src, "hp%d_%d" % (f, u))
-                        else:
-                            sent += write(g, T, topo, core, T.cores[d], T["win%d" % f][:, c0:c0 + PW], src, "aw%d" % f)
-            if relay == core:
-                for f in FAR:
-                    frm = rt[(r + f) % N][k][0]
-                    for u in range(ROUNDS):
-                        g.wait_ge(T.sem["hp%d_%d" % (f, u)], len(topo.engines(frm, core)))
-                        c0 = (u * NH + k) * PW
-                        s = (f * ROUNDS + u) * PW
-                        sent += write(g, T, topo, core, T.cores[r], T["win%d" % f][:, c0:c0 + PW], T.piece[:, s:s + PW], "aw%d" % f)
+        for k, ps in PIECES.items():
+            a, relay = rt[r][k]
+            todo = [(f, j) for f in FAR for j in range(len(ps)) if f in ps[j][5]]
+            seen = set()
+            for f, j in todo:
+                i, b, c0, w, p0, fs = ps[j]
+                name, slot = "%s%d" % (b, f), FAR.index(f) * PT + p0
+                if a == core:
+                    if j not in seen:
+                        seen.add(j)
+                        g.wait_ge(T.sem["hp%d" % j], [len(en) for h, en in feeds(T, topo, r, i) if h == k][0])
+                    if relay is None:
+                        sent += write(g, T, topo, core, T.cores[(r - f) % N], T[name][:, c0:c0 + w], T.piece[:, p0:p0 + w], name,
+                                      AENG if k[0] == "a" else None)
+                        continue
+                    for u, (x, y) in parts(b, w):
+                        sent += write(g, T, topo, core, rt[(r - f) % N][k][1], T.piece[:, slot + x:slot + y], T.piece[:, p0 + x:p0 + y],
+                                      "hr%d_%d_%d" % (f, j, u))
+                if relay == core:
+                    for u, (x, y) in parts(b, w):
+                        g.wait_ge(T.sem["hr%d_%d_%d" % (f, j, u)], len(topo.engines(rt[(r + f) % N][k][0], core)))
+                        sent += write(g, T, topo, core, T.cores[r], T[name][:, c0 + x:c0 + y], T.piece[:, slot + x:slot + y], name)
     if sent:
         g.wait_ge(T.sem.sent, sent)
 
 
 def far_in(h):
-    return h > 0 and PLACE[h] != PLACE[h - 1]
+    return 0 < h < N and PLACE[h] != PLACE[h - 1]
 
 
 def rank_program(g, core, T, topo):
@@ -142,7 +156,7 @@ def rank_program(g, core, T, topo):
     def deps(q, R, W):
         toks = []
         for k in R:
-            toks += wr.get(k, [])
+            toks += wr[k]
         for k in W:
             toks += wr.get(k, []) + rd.get(k, [])
         need(q, toks)
@@ -184,8 +198,11 @@ def rank_program(g, core, T, topo):
             return lambda: S.activation(out, in_, F.Copy)
         return lambda: S.activation(out, in_, F.Identity, scale=scale)
 
-    def ramp(out, pattern, base):
-        return lambda: g.iota(out, pattern, base, 0, allow_small_or_imprecise_dtypes=True)
+    def keep(out, in_, *counts):
+        return lambda: g.affine_select(out, in_, [[0, n] for n in counts], A.is_equal, 0.0, 0, 0)
+
+    def ramp(out, pattern, base, step=0):
+        return lambda: g.iota(out, pattern, base, step, allow_small_or_imprecise_dtypes=True)
 
     def send(dst_rank, out, in_, sem, R):
         deps("g", R, [])
@@ -193,172 +210,185 @@ def rank_program(g, core, T, topo):
 
     far_inc = len(topo.engines(core, T.cores[(rank + 1) % N]))
 
-    op("v", [], ["bx"], ms(T.bx[32:64, :], 1))
-    S.dma_start(T.sxy[:, 0:2], T.sx[:]).then_inc(T.sem.lh, 16)
-    S.dma_start(T.sxy[:, 2:4], T.sy[:]).then_inc(T.sem.lh, 16)
+    S.dma_start(T.sxy[:, 0:2], T.sx[:]).then_inc(T.sem.ls, 16)
+    S.dma_start(T.sxy[:, 2:4], T.sy[:]).then_inc(T.sem.ls, 16)
+    g.sync.dma_start(T.bx[32:56, :], T.box[:]).then_inc(T.sem.lb, 16)
     g.sync.dma_start(T.hd[:], T.head[:]).then_inc(T.sem.lh, 16)
-    deps("y", [], ["bx"])
-    g.sync.dma_start(T.bx[40:64, :], T.box[:]).then_inc(T.sem.lb, 16)
     g.sync.dma_start(T.win0[:, 0:C], T.pyr[:]).then_inc(T.sem.lp, 16)
     wr["bx"] = [("lb", 16)]
-    wr["in"] = [("lh", 48)]
+    wr["sxy"] = [("ls", 32)]
+    wr["hd"] = [("lh", 16)]
     wr["win0"] = [("lp", 16)]
     for f in FAR:
-        wr["win%d" % f] = [("aw%d" % f, far_inc * NH * ROUNDS)]
-        wr["par%d" % f] = [("ap%d" % f, far_inc)]
+        for b in WIDE:
+            n = sum({"a": AENG, "b": far_inc, "m": far_inc * len(parts(b, p[3]))}[k[0]]
+                    for k, ps in PIECES.items() for p in ps if p[1] == b and f in p[5])
+            wr["%s%d" % (b, f)] = [("%s%d" % (b, f), n + sum(far_inc for _, e, i in DIRECT if e == f and PLAN[i][0] == b))]
+
+    def feed(buf, when):
+        for i, (b, w, names, pool, fs, at) in enumerate(PLAN):
+            if names and (b, at) == (buf, when):
+                deps("g", [b + "0"] + ["pad"] * (b == "win"), [])
+                tr = []
+                for k, en in feeds(T, topo, rank, i):
+                    j = [p[0] for p in PIECES[k]].index(i)
+                    c0, w, p0 = PIECES[k][j][2:5]
+                    rid, pid = topo.addr(routes(T, topo)[rank][k][0], core)
+                    tr.append(RemoteDMATransfer(dst_ids=[DstId(rid=rid, pnc=pid)], dma_engine_mask=sum(1 << e for e in en),
+                                                remote_sem=T.sem["hp%d" % j], src=T[b + "0"][:, c0:c0 + w], dst=T.piece[:, p0:p0 + w]))
+                    sent[0] += len(en)
+                g.remote_dma_fused(tr, local_sem=T.sem.sent)
+        for at, f, i in DIRECT:
+            b, lo, hi = SPAN[i]
+            if (b, at) == (buf, when):
+                send(rank - f, T["%s%d" % (b, f)][:, lo:hi], T[b + "0"][:, lo:hi], "%s%d" % (b, f), [b + "0"] + ["pad"] * (b == "win"))
 
     X_, Y_, S_, O_ = slice(8, 32, 3), slice(9, 32, 3), slice(10, 32, 3), slice(0, 8)
-    fm = T.fm
-    op("g", [], ["pc"], lambda: g.iota(T.pc[:, 0:1], [[0, 1]], 0, 1))
-    op("g", [], ["gcol"], ramp(T.gcol[:, :, 0:8], [[0, 4], [1, 8]], 0), ramp(T.gcol[:, :, 8:32], [[0, 4], [1, 8], [0, 3]], 0))
-    op("v", [], ["ones"], ms(T.ones[:], 1.0))
-    op("v", ["pc"], ["pc2"], ts(T.pc[:, 1:2], T.pc[:, 0:1], 4, A.arith_shift_right), ts(T.pc[:, 2:3], T.pc[:, 0:1], 31, A.bitwise_and))
-    op("v", [], ["tab0"], ms(T.tab[:], 0.0))
-    op("v", ["pc2"], ["pf"], cp(T.pf[:, 0:1], T.pc[:, 1:2]), ts(T.pf[:, 1:2], T.pc[:, 2:3], -10.0, A.add))
-    op("g", [], ["rcol"], ramp(T.rcol[:], [[0, 4], [1, 32]], -10))
-    op("g", ["ones"], ["ident"], lambda: g.affine_select(T.ident[:], T.ones[:], [[-1, 128]], A.is_equal, 0.0, 0, 1))
-    op("v", ["pf", "gcol"], ["bd"], ts(T.bd[:], T.gcol[:], T.pf[:, 0:1], A.is_equal))
-    op("v", ["pf", "gcol"], ["prs"], ts(T.prs[:], T.gcol[0:64], 3.0, A.mult, T.pf[0:64, 1:2], A.is_equal))
-    op("v", ["pf", "rcol"], ["prr"], ts(T.prr[:], T.rcol[:], T.pf[0:64, 1:2], A.is_equal))
-    tabs = []
-    for k, sl, tb in ((4, O_, [1.5 * 2.0 ** 29 * b for b in BJ]), (0, S_, [4 * a for a in AJ]), (2, S_, [b / 16 for b in BJ]), (3, X_, BJ), (3, O_, KJ),
-                      (1, Y_, [64 * a for a in AJ]), (1, O_, [2 * a - 32 * b for a, b in zip(AJ, BJ)])):
-        tabs += [(T.tab[:, k, j, sl], T.bd[:, j, sl], tb[j]) for j in range(4)]
-    part("s", ["bd", "tab0"], "tab", *[act(*t) for t in tabs[TAB_ON_V:]])
-    op("v", ["prs"], ["fm2"], ms(fm[:, 2, 0, :], 0.0), ts(fm[:, 2, 1:4, :], T.prs[:, 1:4, :], 64.0, A.mult))
-    op("v", ["prs", "prr"], ["fm"],
-       ts(fm[:, 0, :, X_], T.prs[:, :, X_], -1.0, A.mult), ts(fm[:, 0, :, Y_], T.prs[:, :, Y_], -1.0, A.mult), cp(fm[:, 0, :, S_], T.prs[:, :, S_]),
-       cp(fm[:, 1, :, X_], T.prr[:, :, X_]), cp(fm[:, 1, :, Y_], T.prr[:, :, Y_]), ms(fm[:, 1, :, S_], 0.0), ms(fm[:, 0:2, :, O_], 0.0))
-    op("g", ["ident"], ["fm2"], ramp(fm[32:33, 2, 0, :], [[0, 32]], 64),
-       *[ramp(fm[32:33, 2, j, :], [[0, 32]], -64 * (191 + CUTS[j - 1])) for j in (1, 2, 3)])
-    op("g", [], ["fm"], ramp(fm[32:33, 0:2], [[-448, 2], [0, 128]], 256))
-    op("g", [], ["fm"], ramp(fm[32:33, 0:2, :, S_], [[256, 2], [0, 32]], -192), ramp(fm[32:33, 1, :, O_], [[0, 32]], 1))
-    op("v", ["bd"], ["mz"], ts(T.mz[:], T.bd[:, 0, 0:8], 1.0 / 512, A.mult))
-    op("v", ["in"], ["par0"], cp(T.par0[:, 24:28], T.sxy[:]), cp(T.par0[:, 0:24], T.hd[:]))
-    part("v", ["bd", "tab0"], "tabv", *[ts(o, i, v, A.mult) for o, i, v in tabs[:TAB_ON_V]])
-    op("p", ["tabv", "ident", "ones"], ["pi1"], mm(T.pi1[:, 0:128], T.tab[:, 4], T.ident[:], True, True),
-       mm(T.pi1[:, 128:128 + NM], T.tab[:, 0], T.ones[:, 0:NM], True, True))
-    wr["tab"] = wr["tab"] + wr["tabv"]
-    op("v", [], ["d1"], ms(T.d1[:], 0.0))
-    op("v", ["bx"], ["ee-1"], ms(T.ee[0:32, 512:640], 192.0), cp(T.ee[32:64, 512:640], T.bx[32:64, :]))
-    op("v", [], ["pi1", "is2", "mg"], ts(T.is2[:], T.pi1[:, 128:128 + NM], 0.0, A.not_equal, -4.0, A.mult),
-       cp(T.mg[:, 0:128], T.pi1[:, 0:128]), ts(T.mg[:, 128:256], T.pi1[:, 0:128], -1.0, A.mult))
-    op("v", ["is2"], ["d1"], ts(T.d1[:, 0::4], T.is2[:], 60.0, A.add), ts(T.d1[:, 1::4], T.is2[:], 8.0, A.add))
-    op("v", [], ["pad"], ms(T.win0[:, C:CP], 0.0))
+    fm, tab, gc, M1 = T.fm, T.tab, T.gcol, 1.5 * 2.0 ** 23
 
-    for f in FAR:
-        send(rank - f, T["par%d" % f][:], T.par0[:], "ap%d" % f, ["par0"])
-
-    def frame_diag(f):
-        par = T["par%d" % f]
-        op("s", ["par%d" % f, "ident"], ["dg"], *[act(T.dg[:, 128 * k:128 * k + 128], T.ident[:], par[:, 24 + k:25 + k]) for k in range(4)])
-
-    def frame_lists(f):
-        op("p", ["dg", "tab", "ident"], ["pu0"],
-           *[mm(T.pu0[:, 128 * k:128 * k + 128], T.tab[:, (2 if k < 2 else 0) + i], (T.dg[:, 128 * k:128 * k + 128] if i == 0 else T.ident[:]),
-                i == 0, i == 1) for k in range(4) for i in range(2)])
-
-    def frame_copy(f):
-        op("s", [], ["pu0", "im%d" % f], act(T["im%d" % f][:], T.pu0[:]))
-
-    def frame_head(f, ks):
-        par, wz = T["par%d" % f], T["wz%d" % f]
-        part("s", ["par%d" % f, "mz"], "wz%d" % f, *[act(wz[:, 64 + 24 * k:88 + 24 * k], par[:, 0:24], T.mz[:, k:k + 1]) for k in ks])
+    def rows(out, cols, t, v):
+        return ts(out, cols, T.pf[0:64, 1 + t:2 + t], A.is_equal, v, A.mult)
 
     def forms(bank, e, n, R, fresh):
-        op("p", R + ["fm", "fm2"], [bank], *[mm(T[bank][:, k:4 * n:4], fm[:, (k + 2) % 3], e, True, True) for k in range(0 if fresh else 1, 4)])
+        op("p", R + ["fm"], [bank], *[mm(T[bank][:, k:4 * n:4], fm[:, (k + 2) % 3], e, True, True) for k in range(0 if fresh else 1, 4)])
 
     def update(bank, c0, out, n, key, W):
         op("v", ["d1"], W + [key], lambda: V.tensor_tensor_scan(out, T[bank][:, c0:c0 + 4 * n], T.d1[:, 0:4 * n], 0.0, A.min, A.max))
 
     def first(b):
-        lo, hi = 4 * B0[b], 4 * (B0[b] + BATCH[b])
-        need("v", formed)
-        update("pu1", lo, T.ri0[:, lo:hi], BATCH[b], ("ri", 0, b), [])
+        lo, hi = 4 * B0[0][b], 4 * (B0[0][b] + BATCH[0][b])
+        need("v", wr["pu1"])
+        update("pu1", lo, T.ri0[:, lo:hi], BATCH[0][b], ("r", 0, b), [])
 
     def fills(i):
-        if i == 0:
-            op("v", [], ["bias"], ms(T.bias[0:3, 8:32], 2.0 ** -10), ms(T.bias[0:3, 0:8], 0.0))
-            part("v", [], "pm", ms(T.pm[:, 0::4], 0.0), ms(T.pm[:, 1::4], 256.0))
-            op("v", [], ["bias"], ms(T.bias[0:2, 8:32], -0.5))
-            part("v", [], "wz0", ms(T.wz0[:, 0:64], 0.0))
-            op("v", [], ["bias"], ms(T.bias[0:1, 8:32], 192.0))
-        else:
-            part("v", [], "pm", ms(T.pm[:, 2::4], 256.0), ms(T.pm[:, 3::4], 256.0))
-            op("v", [], ["lim"], ms(T.lim[0:32, 0:1], 180.0), ms(T.lim[32:64, 0:1], 0.0), ms(T.lim[0:32, 1:2], 204.0), ms(T.lim[32:64, 1:2], 255.0))
-            for f in FAR:
-                part("v", [], "wz%d" % f, ms(T["wz%d" % f][:, 0:64], 0.0))
+        op("v", [], ["bias"], ms(T.bias[0:3 - i, :], (2.0 ** -10, -0.5, 192.0)[i]))
+        part("v", [], "pm", *[ms(T.pm[:, PM_G + k::4], 256.0 * k) for k in ((0,), (1, 2), (3,))[i]])
 
-    frame_diag(0)
-    frame_lists(0)
-    forms("pu1", T.ee[:, 512:640], B, ["ee-1"], True)
-    formed = wr["pu1"]
-    frame_head(0, range(4))
-    frame_copy(0)
-    frame_head(0, range(4, 8))
-    first(0)
-    first(1)
+    def diag(q, k):
+        d, p = T.dg[:, 128 * k:128 * k + 128], T.par[:, k:k + 1]
+        op(q, ["par", "ident"], [("dg", k)], act(d, T.ident[:], p) if q == "s" else ts(d, T.ident[:], p, A.mult))
+
+    def lists(bank, m, ks):
+        for k in ks:
+            out = T[bank][:, 128 * (k % 2):128 * (k % 2) + 128]
+            part("p", [("dg", k), "tab", "ident"], bank, mm(out, tab[:, m, 0:128], T.dg[:, 128 * k:128 * k + 128], True, False),
+                 mm(out, tab[:, m + 1, 1 + m // 2:129 + m // 2], T.ident[:], False, True))
+
+    op("g", [], ["pc"], ramp(T.pc[:, 0:1], [[0, 1]], -15, 2))
+    op("g", [], ["gcol0"], ramp(gc[:, :, O_], [[0, 4], [1, 8]], 0))
+    op("v", [], ["tab0"], ms(tab[:], 0.0))
+    op("v", ["pc"], ["pf"], ts(T.pf[:, 0:1], T.pc[:, 0:1], 32 * M1, A.add, 32 * M1, A.subtract))
+    op("v", [], ["ones"], ms(T.ones[:], 1.0))
+    op("v", ["pf", "gcol0"], ["bd"], ts(T.bd[:], gc[:, 0:2, O_], 32.0, A.mult, T.pf[:, 0:1], A.is_equal))
+    part("g", [], "pc3", ramp(T.pc[0:32, 1:4], [[-1, 3]], -8, 1))
+    op("g", [], ["gcol"], ramp(gc[0:64, :, 8:32], [[0, 4], [1, 8], [0, 3]], 0))
+    op("g", ["ones"], ["ident"], lambda: g.affine_select(T.ident[:], T.ones[:], [[-1, 128]], A.is_equal, 0.0, 0, 1))
+    op("v", [], ["fm0", "ee0", "d1"], ms(fm[0:64, 1:3], 0.0), ms(T.ee[0:64, :], 192.0), ms(T.ee[64:65, :], 1.0), ms(T.d1[:], 0.0))
+    op("v", [], ["fmc"], ms(fm[64:65, 0], 256.0), ms(fm[64:65, 1], -192.0))
+    part("v", [], "wz0", ms(T.wz0[:, 0:64], 0.0))
+    op("v", ["bd"], ["mz"], ts(T.mz[:], T.bd[:, 0], 1.0 / 512, A.mult))
+    part("s", ["bd", "tab0"], "tabm", *[act(tab[:, 4, 32 * j:32 * j + 8], T.bd[:, 0], M1 * 64 * BJ[j]) for j in range(4)])
+    for j in range(4):
+        c = 32 * j
+        part("s", [], "tab", act(tab[:, 0:2, c + 10:c + 32:3], T.bd[:], 64 * AJ[j]), act(tab[:, 1, c + 1:c + 9], T.bd[:, 0], 2 * AJ[j] - 32 * BJ[j]),
+             act(tab[:, 2:4, c + 10:c + 32:3], T.bd[:], BJ[j]), act(tab[:, 3, c + 2:c + 10], T.bd[:, 0], KJ[j]))
+    op("p", ["tabm", "ident"], ["pi1"], mm(T.pi1[:, 0:128], tab[:, 4, 0:128], T.ident[:], True, True))
+    part("g", ["ident"], "pc3", ramp(T.pc[32:64, 1:4], [[-1, 3]], 0, 1))
+    part("g", [], "lim", ramp(T.lim[32:64, :], [[255, 2]], 0))
+    op("g", [], ["fmd"], ramp(fm[64:65, 2, 0, :], [[0, 32]], 64), ramp(fm[64:65, 2, 3, :], [[0, 32]], -64 * (191 + CUTS[2])),
+       ramp(fm[64:65, 2, 1:3, :], [[-64 * (CUTS[1] - CUTS[0]), 2], [0, 32]], -64 * (191 + CUTS[0])))
+    op("g", [], ["fmc"], ramp(fm[64:65, 0:2, :, S_], [[256, 2], [0, 32]], -192), ramp(fm[64:65, 1, :, O_], [[0, 32]], 1))
+    op("v", ["pc3"], ["pf3"], ts(T.pf[0:64, 1:4], T.pc[0:64, 1:4], 1.0 / 3, A.mult))
+    op("v", ["sxy"], ["par"], ts(T.par[:], T.sxy[:], 1.0 / 16, A.mult))
+    op("v", ["bx"], ["ee0"], cp(T.ee[32:56, :], T.bx[32:56, :]))
+    op("v", ["pf3", "gcol", "gcol0"], ["fm"], rows(fm[0:64, 0], gc[0:64], 2, -1.0))
+    op("v", ["fm0"], ["fm1"], rows(fm[0:64, 1, :, X_], gc[0:64, :, X_], 0, 1.0), rows(fm[0:64, 1, :, Y_], gc[0:64, :, Y_], 1, 1.0),
+       rows(fm[0:64, 2, 1:4, :], gc[0:64, 1:4, :], 2, 64.0))
+    op("v", [], ["fm"], rows(fm[0:64, 0, :, S_], gc[0:64, :, S_], 2, 1.0))
+    diag("s", 2)
+    diag("s", 3)
+    part("s", ["hd", "mz"], "wz0", *[act(T.wz0[:, 64 + 24 * k:88 + 24 * k], T.hd[:], T.mz[:, k:k + 1]) for k in range(8)])
+    diag("v", 0)
+    diag("v", 1)
+    op("p", ["fm", "ones"], ["pi0"], mm(T.pi0[:, 0:NM], fm[0:32, 0], T.ones[0:32, 0:NM], True, True))
+    lists("pz0", 0, (2, 3))
+    wr["fm"] = wr["fm"] + wr["fmc"]
+    forms("pu1", T.ee[:], B, ["ee0"], True)
+    lists("pu0", 2, (0, 1))
+    op("v", [], ["pi1", "mg"], cp(T.mg[:, 0:128], T.pi1[:, 0:128]), ts(T.mg[:, 128:256], T.pi1[:, 0:128], -1.0, A.mult))
+    op("v", [], ["pi0", "d1"], ts(T.d1[:, 0::4], T.pi0[:, 0:NM], -2.0, A.mult, 58.0, A.add), ts(T.d1[:, 1::4], T.pi0[:, 0:NM], -2.0, A.mult, 6.0, A.add))
+    need("g", [("cg", cnt["g"])])
+    part("g", [], "pm", ramp(T.pm[:, 0:PM_G], [[0, PM_G // 4], [256, 4]], 0))
+    feed("wz", 0)
+    part("g", [], "lim", ramp(T.lim[0:32, :], [[24, 2]], 180))
+    wr["pad"] = []
+    if CP > C:
+        op("g", [], ["pad"], ramp(T.win0[:, C:CP], [[0, CP - C]], 0))
     fills(0)
+    first(0)
+    op("s", [], ["pz0", "im0"], act(T.im0[:, 256:512], T.pz0[:, 0:256]))
+    op("v", [], ["pu0", "imx"], cp(T.im0[:, 0:256], T.pu0[:, 0:256]))
+    wr["im0"] = wr["im0"] + wr["imx"]
+    fills(1)
+    first(1)
+    fills(2)
 
-    def fwd(u):
-        deps("g", ["win0", "pad"], [])
-        tr = []
-        for k, (a, cross, relay, en) in enumerate(routes(T, topo)[rank]):
-            rid, pid = topo.addr(a, core)
-            c0 = (u * NH + k) * PW
-            tr.append(RemoteDMATransfer(dst_ids=[DstId(rid=rid, pnc=pid)], dma_engine_mask=sum(1 << e for e in en),
-                                        remote_sem=T.sem["hp0_%d" % u], src=T.win0[:, c0:c0 + PW], dst=T.piece[:, u * PW:(u + 1) * PW]))
-            sent[0] += len(en)
-        g.remote_dma_fused(tr, local_sem=T.sem.sent)
+    feed("im", 0)
+    feed("win", 0)
 
-    def rin(s):
-        h, b = divmod(s, NBT)
-        buf = T["ri%d" % h] if (h == 0 or far_in(h)) else T["ro%d" % (h - 1)]
-        key = ("ri", h, b) if (h == 0 or far_in(h)) else ("ro", h - 1, b)
-        return buf, 4 * B0[b] + 3, 4 * (B0[b] + BATCH[b]), key
+    def state(h):
+        return T["ri%d" % h] if (h == 0 or far_in(h)) else T["ro%d" % (h - 1)]
 
-    for h in range(1, N):
-        if far_in(h):
-            for b in range(NBT):
-                wr[("ri", h, b)] = [("ar%d_%d" % (h, b), far_inc)]
+    def made(h, lo, hi):
+        k = max(h - 1, 0)
+        return [("r", h, b) for b in range(len(BATCH[k])) if B0[k][b] < hi and lo < B0[k][b] + BATCH[k][b]]
+
+    for h, b in STEP:
+        if far_in(h + 1):
+            wr[("r", h + 1, b)] = [("ar%d_%d" % (h, b), far_inc)]
 
     def geo(s):
-        h, b = divmod(s, NBT)
-        return h, b, BATCH[b], 2 * (B * h + B0[b])
+        h, b = STEP[s]
+        return h, B0[h][b], BATCH[h][b], 2 * (B * h + B0[h][b])
+
+    def cuts(s):
+        h, b0, n, c = geo(s)
+        k = (VCOLS if b0 else VFIRST)[h] * n // 64 * 2
+        return c, c + max(k - VTWO[h] * n // 64 * 2, 0), c + k, c + 2 * n - LAST[h] * n // 64 * 2, c + 2 * n
 
     def idx(s):
-        h, b, n, c = geo(s)
-        buf, lo, hi, key = rin(s)
-        r, im, bank = buf[:, lo:hi:4], T["im%d" % FR[h]], "pi%d" % (s % 2)
+        h, b0, n, c = geo(s)
+        r, im, bank = state(h)[:, 4 * b0 + 3:4 * (b0 + n):4], T["im%d" % FR[h]], "pi%d" % (s % 2)
         calls = []
         for k in range(2):
             o = T[bank][:, k * n:(k + 1) * n]
             calls += [mm(o, im[:, 256 + 128 * k:384 + 128 * k], r, True, False), mm(o, T.mg[:, 0:128], r, False, False),
                       mm(o, T.mg[:, 128:256], r, False, False), mm(o, im[:, 128 * k:128 * k + 128], r, False, True)]
-        op("p", [key, "im%d" % FR[h], "mg"], [bank], *calls)
-
-    def gather(s, q):
-        h, b, n, c = geo(s)
-        k = VCOLS[h] * n // 64 * 2
-        lo, hi = (c, c + k) if q == "v" else (c + k, c + 2 * n)
-        src = T["win%d" % FR[h]][:, 0:C].indirect(T.off[:, lo:hi])
-        part(q, [("off", s), "win%d" % FR[h]], ("gat", s), (cp if q == "v" else act)(T.gat[:, 16 * lo:16 * hi], src))
+        op("p", made(h, b0, b0 + n) + ["im%d" % FR[h], "mg"], [bank], *calls)
 
     def conv(s):
-        h, b, n, c = geo(s)
+        h, b0, n, c = geo(s)
         bank = "pi%d" % (s % 2)
-        op("v", [], [bank, ("off", s)], ts(T.off[:, c:c + 2 * n], T[bank][:, 0:2 * n], 1.5 * 2.0 ** 23, A.add, 1.5 * 2.0 ** 23, A.subtract))
+        op("v", [], [bank, ("off", s)], ts(T.off[:, c:c + 2 * n], T[bank][:, 0:2 * n], M1, A.add, M1, A.subtract))
 
-    def pool(s):
-        h, b, n, c = geo(s)
-        op("v", [("gat", s), "pm"], [("pool", s)],
-           lambda: V.tensor_tensor_scan(T.pool[:, 16 * c:16 * c + 32 * n], T.pm[:, 0:32 * n], T.gat[:, 16 * c:16 * c + 32 * n], 0.0, A.min, A.max))
+    def gather(s, i):
+        h = STEP[s][0]
+        lo, hi = cuts(s)[i:i + 2]
+        if hi > lo:
+            src = T["win%d" % FR[h]][:, 0:C].indirect(T.off[:, lo:hi])
+            op("vvss"[i], [("off", s), "win%d" % FR[h]], [("gat", s, i)], (act if i > 1 else cp)(T.gat[:, 16 * lo:16 * hi], src))
+
+    def pool(s, i):
+        lo, hi = (cuts(s)[0], cuts(s)[3]) if i == 0 else cuts(s)[3:]
+        if hi > lo:
+            part("v", [("gat", s, j) for j in ((0, 1, 2), (3,))[i] if ("gat", s, j) in wr] + ["pm"], ("pool", s),
+                 lambda: V.tensor_tensor_scan(T.pool[:, 16 * lo:16 * hi], T.pm[:, 0:16 * (hi - lo)], T.gat[:, 16 * lo:16 * hi], 0.0, A.min, A.max))
 
     def head(s):
-        h, b, n, c = geo(s)
-        buf, lo, hi, key = rin(s)
+        h, b0, n, c = geo(s)
+        buf, lo, hi = state(h), 4 * b0 + 3, 4 * (b0 + n)
         bank, wz = "pz%d" % (s % 2), T["wz%d" % FR[h]]
-        op("p", [key, "prr", "bias"], [bank], mm(T[bank][32:64, 0:n], T.prr[0:32, 0], buf[0:32, lo:hi:4], True, True),
+        op("p", made(h, b0, b0 + n) + ["ident", "bias"], [bank], mm(T[bank][32:64, 0:n], T.ident[0:32, 8:40], buf[0:32, lo:hi:4], True, True),
            mm(T[bank][0:32, 0:n], T.bias[0:3, :], buf[0:3, lo:hi:4], True, False))
         calls = []
         for m in range(8):
@@ -368,52 +398,92 @@ def rank_program(g, core, T, topo):
         op("p", [("pool", s), "wz%d" % FR[h]], [bank], *calls)
 
     def moves(s):
-        h, b, n, c = geo(s)
+        h, b0, n, c = geo(s)
         bank = "pz%d" % (s % 2)
-        op("v", ["lim"], [bank, ("ee", s)], ts(T.ee[:, c // 2:c // 2 + n], T[bank][0:64, 0:n], T.lim[:, 0:1], A.max, T.lim[:, 1:2], A.min))
+        op("v", ["lim"], [bank, ("ee", s)], ts(T.ee[0:64, b0:b0 + n], T[bank][0:64, 0:n], T.lim[:, 0:1], A.max, T.lim[:, 1:2], A.min))
+
+    written = {}
 
     def form(s):
-        h, b, n, c = geo(s)
-        forms("pt%d" % (s % 2), T.ee[:, c // 2:c // 2 + n], n, [("ee", s)], s < 2)
+        h, b0, n, c = geo(s)
+        forms("pt%d" % (s % 2), T.ee[:, b0:b0 + n], n, [("ee", s)], written.get(s % 2, 0) < n)
+        written[s % 2] = max(written.get(s % 2, 0), n)
 
     def upd(s):
-        h, b, n, c = geo(s)
-        lo, hi = 4 * B0[b], 4 * (B0[b] + n)
-        update("pt%d" % (s % 2), 0, T["ro%d" % h][:, lo:hi], n, ("ro", h, b), ["pt%d" % (s % 2)])
-        if h + 1 < N and far_in(h + 1):
-            send(rank - PLACE[h] + PLACE[h + 1], T["ri%d" % (h + 1)][:, lo:hi], T["ro%d" % h][:, lo:hi], "ar%d_%d" % (h + 1, b), [("ro", h, b)])
+        h, b0, n, c = geo(s)
+        lo, hi, b = 4 * b0, 4 * (b0 + n), STEP[s][1]
+        key = ("o", h, b) if far_in(h + 1) else ("r", h + 1, b)
+        update("pt%d" % (s % 2), 0, T["ro%d" % h][:, lo:hi], n, key, ["pt%d" % (s % 2)])
+        if far_in(h + 1):
+            send(rank - PLACE[h] + PLACE[h + 1], T["ri%d" % (h + 1)][:, lo:hi], T["ro%d" % h][:, lo:hi], "ar%d_%d" % (h, b), [key])
+            for k in WIDE:
+                feed(k, s + 1)
 
     def store(out, in_, R):
         deps("y", R, [])
         g.sync.dma_start(out, in_).then_inc(T.sem.st, 16)
         stores[0] += 16
 
-    def feats(s, q):
-        h, b, n, c = geo(s)
-        part(q, [("pool", s)], "fb", *[(cp if q == "v" else act)(T.fb[:, :, m, B0[b]:B0[b] + n], T.pool[:, 16 * c + 4 * m + 3:16 * c + 32 * n:16])
-                                       for m in ((0, 1) if q == "v" else (2, 3))])
-        if len(wr["fb"]) == 2 * NBT:
+    def feats(s):
+        h, b0, n, c = geo(s)
+        for q, ms_ in (("g", range(4)),) if STEP[s][1] < FEAT_G else (("v", (0, 1)), ("s", (2, 3))):
+            io = [(T.fb[:, :, m, b0:b0 + n], T.pool[:, 16 * c + 4 * m + 3:16 * c + 32 * n:16]) for m in ms_]
+            part(q, [("pool", s)], "fb", *[keep(o, i, 2, n) if q == "g" else (cp if q == "v" else act)(o, i) for o, i in io])
+        if s == len(STEP) - 1:
             store(T.feat[:], T.fb[:], ["fb"])
 
-    def trail(h):
-        q = "v" if h == N - 1 else "s"
-        name = "ri" if PLACE[h] and PLACE[h + 1] == 0 else "ro"
-        k = h + 1 if name == "ri" else h
-        op(q, [(name, k, b) for b in range(NBT)], [("tb", h)], (cp if q == "v" else act)(T["tb%d" % h][:], T["%s%d" % (name, k)][:, 3::4]))
-        if PLACE[h] and PLACE[h + 1]:
-            send(rank - PLACE[h], T["tl%d" % h][:], T["tb%d" % h][:], "at%d" % h, [("tb", h)])
-            wr[("tl", h)] = [("at%d" % h, far_inc)]
-            store(T.trail[:, 384 * h:384 * h + 384], T["tl%d" % h][8:32, :], [("tl", h)])
+    def trail(h, lo, hi):
+        nb = range(len(BATCH[h]))
+        own = PLACE[h] == 0
+        keys = [("o" if own and far_in(h + 1) else "r", h if own and far_in(h + 1) else h + 1, b) for b in nb if lo <= B0[h][b] < hi]
+        o, i = T["tb%d" % h][0:32, lo:hi], (T["ro%d" % h] if own else T["ri%d" % (h + 1)])[0:32, 4 * lo + 3:4 * hi:4]
+        if h == N - 1 and hi == B:
+            part("v", keys, ("tb", h), cp(o, i))
         else:
+            part("g", keys, ("tb", h), keep(o, i, hi - lo))
+        if hi == B:
             store(T.trail[:, 384 * h:384 * h + 384], T["tb%d" % h][8:32, :], [("tb", h)])
 
-    steps = {"idx": idx, "conv": conv, "gv": lambda s: gather(s, "v"), "gs": lambda s: gather(s, "s"), "pool": pool, "head": head,
-             "moves": moves, "form": form, "upd": upd, "first": first, "fill": fills, "trail": trail, "fwd": fwd,
-             "featv": lambda s: feats(s, "v"), "feats": lambda s: feats(s, "s"), "fdiag": frame_diag, "flist": frame_lists,
-             "fcopy": frame_copy, "fhalf": lambda f: frame_head(f, range(4)), "fhead": lambda f: frame_head(f, range(4, 8))}
-    for word in ORDER.split():
-        name = word.rstrip("0123456789")
-        steps[name](int(word[len(name):]))
+    plan, t, ready = [], 0.0, {}
+
+    def at(when, fn, *a):
+        plan.append((when, len(plan), fn, a))
+        return when
+
+    for s, (h, b) in enumerate(STEP):
+        n = BATCH[h][b]
+        lead, lag = LEAD[4 * h:], LAG[5 * h:5 * h + 5]
+        if h == 0 and b > 1:
+            at(t - max(FIRST_AT, lead[0] + 0.01), first, b)
+        t0 = max([t - lead[0]] + [ready[k] for k in made(h, B0[h][b], B0[h][b] + n) if h])
+        at(t0, idx, s)
+        t0 = at(max(t0, t - lead[1]), conv, s)
+        at(max(t0, t), gather, s, 2)
+        at(max(t0, t), gather, s, 3)
+        t0 = at(max(t0, t - lead[2]), gather, s, 0)
+        t0 = at(max(t0, t - lead[3]), gather, s, 1)
+        t += n / 32
+        at(max(t0, t - LAST[h] * n / 32 / 48 + lag[0]), pool, s, 0)
+        t0 = at(max(t0, t + lag[0]), pool, s, 1)
+        tp = t0
+        for d, fn in zip(lag[1:], (head, moves, form, upd)):
+            t0 = at(max(t0, t + d), fn, s)
+        ready[("r", h + 1, b)] = t0
+        if h == N - 1:
+            at(t0 if b + 1 < len(BATCH[h]) else tp + 0.3, feats, s)
+        if b + 1 == len(BATCH[h]):
+            if h == 1:
+                at(t0 + 1, trail, 0, 0, B)
+                at(t0 + GAP[h] + 3, trail, 1, 0, B)
+            if h == 2:
+                at(t0, trail, h, 0, B)
+            if h == 3:
+                at(ready[("r", N, b - 1)], trail, h, 0, B0[h][b])
+                at(t0, trail, h, B0[h][b], B)
+            if h + 1 < N:
+                t += GAP[h]
+    for when, _, fn, a in sorted(plan, key=lambda e: e[:2]):
+        fn(*a)
 
     g.sync.wait_ge(T.sem.st, stores[0])
     need("y", [("c" + q, cnt[q]) for q in "vspg"])

from concourse.bass import DstId, RemoteDMATransfer
from concourse.mybir import AluOpType as A, ActivationFunctionType as F

N, C, B = 4, 5440, 128
PLACE = (0, 1, 0, 0)
BATCH = ((32, 32, 32, 32), (32, 32, 32, 32), (32, 32, 32, 32), (32, 32, 32, 32))
VCOLS = (16, 16, 18, 16)
VFIRST = (28, 22, 26, 18)
LAST = (0, 0, 0, 0)
VTWO = (0, 0, 0, 0)
GAP = (0.4, 0.4, 0.0)
LEAD = (1.0, 0.5, -0.45, -0.7, 0.4, 0.15, -0.45, -0.7, 0.4, 0.15, -0.65, -0.65, 0.85, 0.45, -0.65, -0.65)
LAG = (-0.15, 0.45, 0.65, 0.7, 0.95, 0.0, 0.9, 0.65, 0.7, 1.1, 0, 0.45, 0.8, 0.9, 1.3, 0, 0.45, 0.8, 0.9, 1.3)
FEAT_G = 3
PLAN = (("wz", 128, "b0 b1", "hi", (2, 3), 0), ("im", 128, "m0 m1 m2 m3", "all", (2, 3), 0), ("win", 640, "m0 m2", "lo", (2, 3), 0), ("win", 720, "m1 m3", "hi", (2, 3), 0), ("win", 720, "b0 b1", "hi", (2, 3), 0), ("win", 480, "", "lo", (), 0), ("win", 800, "", "lo", (), 0))
DIRECT = ((2, 2, 5), (4, 2, 6), (6, 3, 5), (8, 3, 6))
SUB = 3
AENG = 2
PM_G = 384
FIRST_AT = 1.2
SIM = 256
CUTS = (12, 24, 48)
BJ = (1.0, -0.5, -0.25, -0.125)
AJ = (1.0, -0.75, -0.1875, -0.046875)
KJ = (-127.0 / 256, 4096.0, 1024.0, 256.0)
B0 = [[sum(bs[:b]) for b in range(len(bs))] for bs in BATCH]
STEP = [(h, b) for h in range(N) for b in range(len(BATCH[h]))]
FR = [h - PLACE[h] for h in range(N)]
FAR = sorted(set(f for f in FR if f))
NM = max(max(bs) for bs in BATCH)
BF, F32 = "bfloat16", "float32"

PIECES, SPAN, WIDE = {}, [], {}
for _i, (_b, _w, _names, _pool, _fs, _when) in enumerate(PLAN):
    SPAN.append((_b, WIDE.get(_b, 0), WIDE.get(_b, 0) + _w * max(len(_names.split()), 1)))
    for _j, _k in enumerate(_names.split()):
        PIECES.setdefault(_k, []).append((_i, _b, SPAN[_i][1] + _j * _w, _w, sum(p[3] for p in PIECES.get(_k, [])), _fs))
    WIDE[_b] = SPAN[_i][2]
CP = WIDE["win"]
PT = max(sum(p[3] for p in ps) for ps in PIECES.values())
PN = max(len(ps) for ps in PIECES.values())

SCRATCH = {k: ("sbuf", s, d) for k, s, d in (
    ("hd", [128, 24], BF), ("sxy", [128, 4], "int32"), ("bx", [64, 128], "int32"), ("ones", [128, 128], BF), ("ident", [128, 128], BF),
    ("gcol", [128, 4, 32], F32), ("pc", [128, 4], F32), ("pf", [128, 4], F32), ("bd", [128, 2, 8], BF),
    ("mz", [128, 8], F32), ("tab", [128, 5, 132], BF), ("fm", [65, 3, 4, 32], BF),
    ("bias", [4, 32], BF), ("lim", [64, 2], F32), ("mg", [128, 256], BF), ("d1", [128, 4 * NM], BF), ("par", [128, 4], F32),
    ("pm", [128, 32 * NM], BF), ("dg", [128, 512], BF), ("off", [128, 1024], "uint16"), ("gat", [128, 16384], BF), ("pool", [128, 16384], BF),
    ("ee", [65, 128], BF), ("fb", [128, 2, 4, 128], BF), ("piece", [128, len(FAR) * PT], BF))}
for _k in ("pi0", "pi1", "pz0", "pz1", "pt0", "pt1", "pu0", "pu1"):
    SCRATCH[_k] = ("psum", [128, 512], F32)
for _f in [0] + FAR:
    for _k, _w in (("win", CP), ("im", 512), ("wz", 256)):
        SCRATCH["%s%d" % (_k, _f)] = ("sbuf", [128, _w], BF)
for _h in range(N):
    for _k, _w, _d in (("ri", 512, BF), ("ro", 512, BF), ("tb", 128, F32)):
        SCRATCH["%s%d" % (_k, _h)] = ("sbuf", [128, _w], _d)

SEMAPHORES = (["cv", "cs", "cp", "cg", "lp", "lh", "ls", "lb", "sent", "st"] + ["%s%d" % (k, f) for k in WIDE for f in FAR]
              + ["ar%d_%d" % hb for hb in STEP] + ["hp%d" % j for j in range(PN)]
              + ["hr%d_%d_%d" % (f, j, u) for f in FAR for j in range(PN) for u in range(SUB)])


def routes(T, topo):
    out = []
    for c in T.cores:
        mate = [m for m in range(SIM) if topo.mates(c, m)]
        rest = sorted((a for a in topo.cores_of(c) if a != c), key=lambda a: topo.die(a) != topo.die(c))
        cross = [a for a in rest if topo.may_write(a, mate[0])]
        relay = sorted((m for m in mate if topo.may_write(m, c)), key=lambda m: topo.die(m) != topo.die(c))
        hs = {"m%d" % i: (a, relay[i]) for i, a in enumerate(cross)}
        for name, same in (("a", True), ("b", False)):
            hs.update({"%s%d" % (name, i): (a, None)
                       for i, a in enumerate(a for a in rest if a not in cross and (topo.die(a) == topo.die(c)) == same)})
        out.append(hs)
    return out


def feeds(T, topo, r, i):
    c, names = T.cores[r], PLAN[i][2].split()
    low = topo.engines(c, T.cores[(r + 1) % N])
    every = topo.engines(c, routes(T, topo)[r]["a0"][0])
    pool = {"lo": low, "hi": [e for e in every if e not in low], "all": every}[PLAN[i][3]]
    m = len(pool) // len(names)
    return [(k, pool[m * j:m * j + m]) for j, k in enumerate(names)]


def write(g, T, topo, src, dst, out, in_, sem, most=None):
    rid, pid = topo.addr(dst, src)
    en = topo.engines(src, dst)[:most]
    g.remote_dma(out, in_, T.sem[sem], T.sem.sent, pid, rid, sum(1 << e for e in en))
    return len(en)


def parts(b, w):
    n = SUB if b == "win" else 1
    cut = [8 * ((w // 8) * u // n) for u in range(n + 1)]
    return list(enumerate(zip(cut, cut[1:])))


def helper_program(g, core, T, topo):
    rt = routes(T, topo)
    sent = 0
    for r in range(N):
        for k, ps in PIECES.items():
            a, relay = rt[r][k]
            todo = [(f, j) for f in FAR for j in range(len(ps)) if f in ps[j][5]]
            seen = set()
            for f, j in todo:
                i, b, c0, w, p0, fs = ps[j]
                name, slot = "%s%d" % (b, f), FAR.index(f) * PT + p0
                if a == core:
                    if j not in seen:
                        seen.add(j)
                        g.wait_ge(T.sem["hp%d" % j], [len(en) for h, en in feeds(T, topo, r, i) if h == k][0])
                    if relay is None:
                        sent += write(g, T, topo, core, T.cores[(r - f) % N], T[name][:, c0:c0 + w], T.piece[:, p0:p0 + w], name,
                                      AENG if k[0] == "a" else None)
                        continue
                    for u, (x, y) in parts(b, w):
                        sent += write(g, T, topo, core, rt[(r - f) % N][k][1], T.piece[:, slot + x:slot + y], T.piece[:, p0 + x:p0 + y],
                                      "hr%d_%d_%d" % (f, j, u))
                if relay == core:
                    for u, (x, y) in parts(b, w):
                        g.wait_ge(T.sem["hr%d_%d_%d" % (f, j, u)], len(topo.engines(rt[(r + f) % N][k][0], core)))
                        sent += write(g, T, topo, core, T.cores[r], T[name][:, c0 + x:c0 + y], T.piece[:, slot + x:slot + y], name)
    if sent:
        g.wait_ge(T.sem.sent, sent)


def far_in(h):
    return 0 < h < N and PLACE[h] != PLACE[h - 1]


def rank_program(g, core, T, topo):
    rank = T.rank_of(core)
    if rank is None:
        helper_program(g, core, T, topo)
        return
    V, S, P = g.vector, g.scalar, g.tensor
    Q = {"v": V, "s": S, "p": P, "g": g, "y": g.sync}
    cnt = {"v": 0, "s": 0, "p": 0, "g": 0}
    waited, wr, rd = {}, {}, {}
    sent = [0]
    stores = [0]

    def need(q, toks):
        best = {}
        for s, n in toks:
            best[s] = max(best.get(s, 0), n)
        for s, n in best.items():
            if waited.get((q, s), 0) < n:
                Q[q].wait_ge(T.sem[s], n)
                waited[(q, s)] = n

    def deps(q, R, W):
        toks = []
        for k in R:
            toks += wr[k]
        for k in W:
            toks += wr.get(k, []) + rd.get(k, [])
        need(q, toks)

    def done(tok, R, W):
        for k in R:
            rd.setdefault(k, []).append(tok)
        for k in W:
            wr[k] = [tok]
            rd[k] = []

    def op(q, R, W, *calls):
        deps(q, R, W)
        for c in calls:
            c().then_inc(T.sem["c" + q], 1)
            cnt[q] += 1
        done(("c" + q, cnt[q]), R, W)

    def part(q, R, key, *calls):
        op(q, R, [], *calls)
        wr.setdefault(key, []).append(("c" + q, cnt[q]))

    def ts(out, in0, s1, o1, s2=None, o2=None):
        if o2 is None:
            return lambda: V.tensor_scalar(out, in0, s1, None, o1)
        return lambda: V.tensor_scalar(out, in0, s1, s2, o1, o2)

    def ms(ap, v):
        return lambda: V.memset(ap, v)

    def cp(out, in_):
        return lambda: V.tensor_copy(out, in_)

    def mm(out, l, r, a, z):
        return lambda: P.matmul(out, l, r, a, z)

    def act(out, in_, scale=None):
        if scale is None:
            return lambda: S.activation(out, in_, F.Copy)
        return lambda: S.activation(out, in_, F.Identity, scale=scale)

    def keep(out, in_, *counts):
        return lambda: g.affine_select(out, in_, [[0, n] for n in counts], A.is_equal, 0.0, 0, 0)

    def ramp(out, pattern, base, step=0):
        return lambda: g.iota(out, pattern, base, step, allow_small_or_imprecise_dtypes=True)

    def send(dst_rank, out, in_, sem, R):
        deps("g", R, [])
        sent[0] += write(g, T, topo, core, T.cores[dst_rank % N], out, in_, sem)

    far_inc = len(topo.engines(core, T.cores[(rank + 1) % N]))

    S.dma_start(T.sxy[:, 0:2], T.sx[:]).then_inc(T.sem.ls, 16)
    S.dma_start(T.sxy[:, 2:4], T.sy[:]).then_inc(T.sem.ls, 16)
    g.sync.dma_start(T.bx[32:56, :], T.box[:]).then_inc(T.sem.lb, 16)
    g.sync.dma_start(T.hd[:], T.head[:]).then_inc(T.sem.lh, 16)
    g.sync.dma_start(T.win0[:, 0:C], T.pyr[:]).then_inc(T.sem.lp, 16)
    wr["bx"] = [("lb", 16)]
    wr["sxy"] = [("ls", 32)]
    wr["hd"] = [("lh", 16)]
    wr["win0"] = [("lp", 16)]
    for f in FAR:
        for b in WIDE:
            n = sum({"a": AENG, "b": far_inc, "m": far_inc * len(parts(b, p[3]))}[k[0]]
                    for k, ps in PIECES.items() for p in ps if p[1] == b and f in p[5])
            wr["%s%d" % (b, f)] = [("%s%d" % (b, f), n + sum(far_inc for _, e, i in DIRECT if e == f and PLAN[i][0] == b))]

    def feed(buf, when):
        for i, (b, w, names, pool, fs, at) in enumerate(PLAN):
            if names and (b, at) == (buf, when):
                deps("g", [b + "0"] + ["pad"] * (b == "win"), [])
                tr = []
                for k, en in feeds(T, topo, rank, i):
                    j = [p[0] for p in PIECES[k]].index(i)
                    c0, w, p0 = PIECES[k][j][2:5]
                    rid, pid = topo.addr(routes(T, topo)[rank][k][0], core)
                    tr.append(RemoteDMATransfer(dst_ids=[DstId(rid=rid, pnc=pid)], dma_engine_mask=sum(1 << e for e in en),
                                                remote_sem=T.sem["hp%d" % j], src=T[b + "0"][:, c0:c0 + w], dst=T.piece[:, p0:p0 + w]))
                    sent[0] += len(en)
                g.remote_dma_fused(tr, local_sem=T.sem.sent)
        for at, f, i in DIRECT:
            b, lo, hi = SPAN[i]
            if (b, at) == (buf, when):
                send(rank - f, T["%s%d" % (b, f)][:, lo:hi], T[b + "0"][:, lo:hi], "%s%d" % (b, f), [b + "0"] + ["pad"] * (b == "win"))

    X_, Y_, S_, O_ = slice(8, 32, 3), slice(9, 32, 3), slice(10, 32, 3), slice(0, 8)
    fm, tab, gc, M1 = T.fm, T.tab, T.gcol, 1.5 * 2.0 ** 23

    def rows(out, cols, t, v):
        return ts(out, cols, T.pf[0:64, 1 + t:2 + t], A.is_equal, v, A.mult)

    def forms(bank, e, n, R, fresh):
        op("p", R + ["fm"], [bank], *[mm(T[bank][:, k:4 * n:4], fm[:, (k + 2) % 3], e, True, True) for k in range(0 if fresh else 1, 4)])

    def update(bank, c0, out, n, key, W):
        op("v", ["d1"], W + [key], lambda: V.tensor_tensor_scan(out, T[bank][:, c0:c0 + 4 * n], T.d1[:, 0:4 * n], 0.0, A.min, A.max))

    def first(b):
        lo, hi = 4 * B0[0][b], 4 * (B0[0][b] + BATCH[0][b])
        need("v", wr["pu1"])
        update("pu1", lo, T.ri0[:, lo:hi], BATCH[0][b], ("r", 0, b), [])

    def fills(i):
        op("v", [], ["bias"], ms(T.bias[0:3 - i, :], (2.0 ** -10, -0.5, 192.0)[i]))
        part("v", [], "pm", *[ms(T.pm[:, PM_G + k::4], 256.0 * k) for k in ((0,), (1, 2), (3,))[i]])

    def diag(q, k):
        d, p = T.dg[:, 128 * k:128 * k + 128], T.par[:, k:k + 1]
        op(q, ["par", "ident"], [("dg", k)], act(d, T.ident[:], p) if q == "s" else ts(d, T.ident[:], p, A.mult))

    def lists(bank, m, ks):
        for k in ks:
            out = T[bank][:, 128 * (k % 2):128 * (k % 2) + 128]
            part("p", [("dg", k), "tab", "ident"], bank, mm(out, tab[:, m, 0:128], T.dg[:, 128 * k:128 * k + 128], True, False),
                 mm(out, tab[:, m + 1, 1 + m // 2:129 + m // 2], T.ident[:], False, True))

    op("g", [], ["pc"], ramp(T.pc[:, 0:1], [[0, 1]], -15, 2))
    op("g", [], ["gcol0"], ramp(gc[:, :, O_], [[0, 4], [1, 8]], 0))
    op("v", [], ["tab0"], ms(tab[:], 0.0))
    op("v", ["pc"], ["pf"], ts(T.pf[:, 0:1], T.pc[:, 0:1], 32 * M1, A.add, 32 * M1, A.subtract))
    op("v", [], ["ones"], ms(T.ones[:], 1.0))
    op("v", ["pf", "gcol0"], ["bd"], ts(T.bd[:], gc[:, 0:2, O_], 32.0, A.mult, T.pf[:, 0:1], A.is_equal))
    part("g", [], "pc3", ramp(T.pc[0:32, 1:4], [[-1, 3]], -8, 1))
    op("g", [], ["gcol"], ramp(gc[0:64, :, 8:32], [[0, 4], [1, 8], [0, 3]], 0))
    op("g", ["ones"], ["ident"], lambda: g.affine_select(T.ident[:], T.ones[:], [[-1, 128]], A.is_equal, 0.0, 0, 1))
    op("v", [], ["fm0", "ee0", "d1"], ms(fm[0:64, 1:3], 0.0), ms(T.ee[0:64, :], 192.0), ms(T.ee[64:65, :], 1.0), ms(T.d1[:], 0.0))
    op("v", [], ["fmc"], ms(fm[64:65, 0], 256.0), ms(fm[64:65, 1], -192.0))
    part("v", [], "wz0", ms(T.wz0[:, 0:64], 0.0))
    op("v", ["bd"], ["mz"], ts(T.mz[:], T.bd[:, 0], 1.0 / 512, A.mult))
    part("s", ["bd", "tab0"], "tabm", *[act(tab[:, 4, 32 * j:32 * j + 8], T.bd[:, 0], M1 * 64 * BJ[j]) for j in range(4)])
    for j in range(4):
        c = 32 * j
        part("s", [], "tab", act(tab[:, 0:2, c + 10:c + 32:3], T.bd[:], 64 * AJ[j]), act(tab[:, 1, c + 1:c + 9], T.bd[:, 0], 2 * AJ[j] - 32 * BJ[j]),
             act(tab[:, 2:4, c + 10:c + 32:3], T.bd[:], BJ[j]), act(tab[:, 3, c + 2:c + 10], T.bd[:, 0], KJ[j]))
    op("p", ["tabm", "ident"], ["pi1"], mm(T.pi1[:, 0:128], tab[:, 4, 0:128], T.ident[:], True, True))
    part("g", ["ident"], "pc3", ramp(T.pc[32:64, 1:4], [[-1, 3]], 0, 1))
    part("g", [], "lim", ramp(T.lim[32:64, :], [[255, 2]], 0))
    op("g", [], ["fmd"], ramp(fm[64:65, 2, 0, :], [[0, 32]], 64), ramp(fm[64:65, 2, 3, :], [[0, 32]], -64 * (191 + CUTS[2])),
       ramp(fm[64:65, 2, 1:3, :], [[-64 * (CUTS[1] - CUTS[0]), 2], [0, 32]], -64 * (191 + CUTS[0])))
    op("g", [], ["fmc"], ramp(fm[64:65, 0:2, :, S_], [[256, 2], [0, 32]], -192), ramp(fm[64:65, 1, :, O_], [[0, 32]], 1))
    op("v", ["pc3"], ["pf3"], ts(T.pf[0:64, 1:4], T.pc[0:64, 1:4], 1.0 / 3, A.mult))
    op("v", ["sxy"], ["par"], ts(T.par[:], T.sxy[:], 1.0 / 16, A.mult))
    op("v", ["bx"], ["ee0"], cp(T.ee[32:56, :], T.bx[32:56, :]))
    op("v", ["pf3", "gcol", "gcol0"], ["fm"], rows(fm[0:64, 0], gc[0:64], 2, -1.0))
    op("v", ["fm0"], ["fm1"], rows(fm[0:64, 1, :, X_], gc[0:64, :, X_], 0, 1.0), rows(fm[0:64, 1, :, Y_], gc[0:64, :, Y_], 1, 1.0),
       rows(fm[0:64, 2, 1:4, :], gc[0:64, 1:4, :], 2, 64.0))
    op("v", [], ["fm"], rows(fm[0:64, 0, :, S_], gc[0:64, :, S_], 2, 1.0))
    diag("s", 2)
    diag("s", 3)
    part("s", ["hd", "mz"], "wz0", *[act(T.wz0[:, 64 + 24 * k:88 + 24 * k], T.hd[:], T.mz[:, k:k + 1]) for k in range(8)])
    diag("v", 0)
    diag("v", 1)
    op("p", ["fm", "ones"], ["pi0"], mm(T.pi0[:, 0:NM], fm[0:32, 0], T.ones[0:32, 0:NM], True, True))
    lists("pz0", 0, (2, 3))
    wr["fm"] = wr["fm"] + wr["fmc"]
    forms("pu1", T.ee[:], B, ["ee0"], True)
    lists("pu0", 2, (0, 1))
    op("v", [], ["pi1", "mg"], cp(T.mg[:, 0:128], T.pi1[:, 0:128]), ts(T.mg[:, 128:256], T.pi1[:, 0:128], -1.0, A.mult))
    op("v", [], ["pi0", "d1"], ts(T.d1[:, 0::4], T.pi0[:, 0:NM], -2.0, A.mult, 58.0, A.add), ts(T.d1[:, 1::4], T.pi0[:, 0:NM], -2.0, A.mult, 6.0, A.add))
    need("g", [("cg", cnt["g"])])
    part("g", [], "pm", ramp(T.pm[:, 0:PM_G], [[0, PM_G // 4], [256, 4]], 0))
    feed("wz", 0)
    part("g", [], "lim", ramp(T.lim[0:32, :], [[24, 2]], 180))
    wr["pad"] = []
    if CP > C:
        op("g", [], ["pad"], ramp(T.win0[:, C:CP], [[0, CP - C]], 0))
    fills(0)
    first(0)
    op("s", [], ["pz0", "im0"], act(T.im0[:, 256:512], T.pz0[:, 0:256]))
    op("v", [], ["pu0", "imx"], cp(T.im0[:, 0:256], T.pu0[:, 0:256]))
    wr["im0"] = wr["im0"] + wr["imx"]
    fills(1)
    first(1)
    fills(2)

    feed("im", 0)
    feed("win", 0)

    def state(h):
        return T["ri%d" % h] if (h == 0 or far_in(h)) else T["ro%d" % (h - 1)]

    def made(h, lo, hi):
        k = max(h - 1, 0)
        return [("r", h, b) for b in range(len(BATCH[k])) if B0[k][b] < hi and lo < B0[k][b] + BATCH[k][b]]

    for h, b in STEP:
        if far_in(h + 1):
            wr[("r", h + 1, b)] = [("ar%d_%d" % (h, b), far_inc)]

    def geo(s):
        h, b = STEP[s]
        return h, B0[h][b], BATCH[h][b], 2 * (B * h + B0[h][b])

    def cuts(s):
        h, b0, n, c = geo(s)
        k = (VCOLS if b0 else VFIRST)[h] * n // 64 * 2
        return c, c + max(k - VTWO[h] * n // 64 * 2, 0), c + k, c + 2 * n - LAST[h] * n // 64 * 2, c + 2 * n

    def idx(s):
        h, b0, n, c = geo(s)
        r, im, bank = state(h)[:, 4 * b0 + 3:4 * (b0 + n):4], T["im%d" % FR[h]], "pi%d" % (s % 2)
        calls = []
        for k in range(2):
            o = T[bank][:, k * n:(k + 1) * n]
            calls += [mm(o, im[:, 256 + 128 * k:384 + 128 * k], r, True, False), mm(o, T.mg[:, 0:128], r, False, False),
                      mm(o, T.mg[:, 128:256], r, False, False), mm(o, im[:, 128 * k:128 * k + 128], r, False, True)]
        op("p", made(h, b0, b0 + n) + ["im%d" % FR[h], "mg"], [bank], *calls)

    def conv(s):
        h, b0, n, c = geo(s)
        bank = "pi%d" % (s % 2)
        op("v", [], [bank, ("off", s)], ts(T.off[:, c:c + 2 * n], T[bank][:, 0:2 * n], M1, A.add, M1, A.subtract))

    def gather(s, i):
        h = STEP[s][0]
        lo, hi = cuts(s)[i:i + 2]
        if hi > lo:
            src = T["win%d" % FR[h]][:, 0:C].indirect(T.off[:, lo:hi])
            op("vvss"[i], [("off", s), "win%d" % FR[h]], [("gat", s, i)], (act if i > 1 else cp)(T.gat[:, 16 * lo:16 * hi], src))

    def pool(s, i):
        lo, hi = (cuts(s)[0], cuts(s)[3]) if i == 0 else cuts(s)[3:]
        if hi > lo:
            part("v", [("gat", s, j) for j in ((0, 1, 2), (3,))[i] if ("gat", s, j) in wr] + ["pm"], ("pool", s),
                 lambda: V.tensor_tensor_scan(T.pool[:, 16 * lo:16 * hi], T.pm[:, 0:16 * (hi - lo)], T.gat[:, 16 * lo:16 * hi], 0.0, A.min, A.max))

    def head(s):
        h, b0, n, c = geo(s)
        buf, lo, hi = state(h), 4 * b0 + 3, 4 * (b0 + n)
        bank, wz = "pz%d" % (s % 2), T["wz%d" % FR[h]]
        op("p", made(h, b0, b0 + n) + ["ident", "bias"], [bank], mm(T[bank][32:64, 0:n], T.ident[0:32, 8:40], buf[0:32, lo:hi:4], True, True),
           mm(T[bank][0:32, 0:n], T.bias[0:3, :], buf[0:3, lo:hi:4], True, False))
        calls = []
        for m in range(8):
            a = 16 * (c + (m // 4) * n) + 4 * (m % 4) + 3
            calls.append(mm(T[bank][0:32, 0:n], wz[:, m::8], T.pool[:, a:a + 16 * (n - 1) + 1:16], False, m == 7))
        wr.pop(bank)
        op("p", [("pool", s), "wz%d" % FR[h]], [bank], *calls)

    def moves(s):
        h, b0, n, c = geo(s)
        bank = "pz%d" % (s % 2)
        op("v", ["lim"], [bank, ("ee", s)], ts(T.ee[0:64, b0:b0 + n], T[bank][0:64, 0:n], T.lim[:, 0:1], A.max, T.lim[:, 1:2], A.min))

    written = {}

    def form(s):
        h, b0, n, c = geo(s)
        forms("pt%d" % (s % 2), T.ee[:, b0:b0 + n], n, [("ee", s)], written.get(s % 2, 0) < n)
        written[s % 2] = max(written.get(s % 2, 0), n)

    def upd(s):
        h, b0, n, c = geo(s)
        lo, hi, b = 4 * b0, 4 * (b0 + n), STEP[s][1]
        key = ("o", h, b) if far_in(h + 1) else ("r", h + 1, b)
        update("pt%d" % (s % 2), 0, T["ro%d" % h][:, lo:hi], n, key, ["pt%d" % (s % 2)])
        if far_in(h + 1):
            send(rank - PLACE[h] + PLACE[h + 1], T["ri%d" % (h + 1)][:, lo:hi], T["ro%d" % h][:, lo:hi], "ar%d_%d" % (h, b), [key])
            for k in WIDE:
                feed(k, s + 1)

    def store(out, in_, R):
        deps("y", R, [])
        g.sync.dma_start(out, in_).then_inc(T.sem.st, 16)
        stores[0] += 16

    def feats(s):
        h, b0, n, c = geo(s)
        for q, ms_ in (("g", range(4)),) if STEP[s][1] < FEAT_G else (("v", (0, 1)), ("s", (2, 3))):
            io = [(T.fb[:, :, m, b0:b0 + n], T.pool[:, 16 * c + 4 * m + 3:16 * c + 32 * n:16]) for m in ms_]
            part(q, [("pool", s)], "fb", *[keep(o, i, 2, n) if q == "g" else (cp if q == "v" else act)(o, i) for o, i in io])
        if s == len(STEP) - 1:
            store(T.feat[:], T.fb[:], ["fb"])

    def trail(h, lo, hi):
        nb = range(len(BATCH[h]))
        own = PLACE[h] == 0
        keys = [("o" if own and far_in(h + 1) else "r", h if own and far_in(h + 1) else h + 1, b) for b in nb if lo <= B0[h][b] < hi]
        o, i = T["tb%d" % h][0:32, lo:hi], (T["ro%d" % h] if own else T["ri%d" % (h + 1)])[0:32, 4 * lo + 3:4 * hi:4]
        if h == N - 1 and hi == B:
            part("v", keys, ("tb", h), cp(o, i))
        else:
            part("g", keys, ("tb", h), keep(o, i, hi - lo))
        if hi == B:
            store(T.trail[:, 384 * h:384 * h + 384], T["tb%d" % h][8:32, :], [("tb", h)])

    plan, t, ready = [], 0.0, {}

    def at(when, fn, *a):
        plan.append((when, len(plan), fn, a))
        return when

    for s, (h, b) in enumerate(STEP):
        n = BATCH[h][b]
        lead, lag = LEAD[4 * h:], LAG[5 * h:5 * h + 5]
        if h == 0 and b > 1:
            at(t - max(FIRST_AT, lead[0] + 0.01), first, b)
        t0 = max([t - lead[0]] + [ready[k] for k in made(h, B0[h][b], B0[h][b] + n) if h])
        at(t0, idx, s)
        t0 = at(max(t0, t - lead[1]), conv, s)
        at(max(t0, t), gather, s, 2)
        at(max(t0, t), gather, s, 3)
        t0 = at(max(t0, t - lead[2]), gather, s, 0)
        t0 = at(max(t0, t - lead[3]), gather, s, 1)
        t += n / 32
        at(max(t0, t - LAST[h] * n / 32 / 48 + lag[0]), pool, s, 0)
        t0 = at(max(t0, t + lag[0]), pool, s, 1)
        tp = t0
        for d, fn in zip(lag[1:], (head, moves, form, upd)):
            t0 = at(max(t0, t + d), fn, s)
        ready[("r", h + 1, b)] = t0
        if h == N - 1:
            at(t0 if b + 1 < len(BATCH[h]) else tp + 0.3, feats, s)
        if b + 1 == len(BATCH[h]):
            if h == 1:
                at(t0 + 1, trail, 0, 0, B)
                at(t0 + GAP[h] + 3, trail, 1, 0, B)
            if h == 2:
                at(t0, trail, h, 0, B)
            if h == 3:
                at(ready[("r", N, b - 1)], trail, h, 0, B0[h][b])
                at(t0, trail, h, B0[h][b], B)
            if h + 1 < N:
                t += GAP[h]
    for when, _, fn, a in sorted(plan, key=lambda e: e[:2]):
        fn(*a)

    g.sync.wait_ge(T.sem.st, stores[0])
    need("y", [("c" + q, cnt[q]) for q in "vspg"])
    g.wait_ge(T.sem.sent, sent[0])
